import numpy as np, ml_dtypes
CORES = [40,41,42,43,44,45,46,47]
N = 8
import mx_ref
BF = ml_dtypes.bfloat16
def pick(q, e):
    c = np.concatenate([q[0].reshape(128, -1, 4), np.zeros((128, 1, 4), np.uint8)], axis=1); s = np.concatenate([q[1], np.ones((16, 1), np.uint8)], axis=1)
    return (np.ascontiguousarray(c[:, e].reshape(128, -1)), np.ascontiguousarray(s[:, e]))
def join(*qs):
    return (np.concatenate([q[0] for q in qs], axis=1), np.concatenate([q[1] for q in qs], axis=1))
def put(q, e, v):
    c, s = q[0].reshape(128, -1, 4).copy(), q[1].copy(); c[:, e] = v[0].reshape(128, -1, 4); s[:, e] = v[1]
    return (c.reshape(128, -1), s)
def pk(c, s):
    return (np.ascontiguousarray(c), mx_ref.live(s))
def emit(q):
    return q[0], q[1]
def decode(q):
    o = []
    for b in range(4):
        e = np.zeros((128, 128, 4), np.float32); e[np.arange(128), np.arange(128), b] = 1
        o.append(mx_ref.matmul(mx_ref.quantize(e.reshape(128, 512).astype(BF)), q))
    return np.stack(o, axis=2).reshape(128, -1)
def f(rng, *shape):
    return mx_ref.flush((rng.standard_normal(shape, dtype=np.float32) * np.exp2(rng.integers(-2, 3, shape[:-1] + (1,)))).astype(BF))
def wide(rng, *shape, cols=0):
    v = rng.standard_normal(shape, dtype=np.float32) * np.exp2(rng.integers(-12, 13, shape)).astype(np.float32)
    if cols: v *= np.repeat(np.exp2(rng.integers(-cols, cols + 1, shape[:-2] + (1, shape[-1] // 4))) * (rng.random(shape[:-2] + (1, shape[-1] // 4)) > 0.0625), 4, axis=-1).astype(np.float32)
    return mx_ref.flush(v.astype(BF))
T, CAPP = 128, 32
def quads(q, e):
    c = np.concatenate([q[0].reshape(128, -1, 4), np.zeros((128, 1, 4), np.uint8)], axis=1); s = np.concatenate([q[1], np.ones((16, 1), np.uint8)], axis=1)
    return (np.concatenate([c[32 * h:32 * h + 32][:, e[h]] for h in range(4)]).reshape(128, -1), np.concatenate([s[4 * h:4 * h + 4][:, e[h]] for h in range(4)]))
def level(b, z):
    n, e = z[1].shape[1], []
    for h in range(4):
        only = np.where(np.arange(4)[:, None] == h, np.arange(n)[None, :], -1)
        e.append(np.argmax(mx_ref.matmul(b, quads(z, only)) + np.float32(0), axis=0))
    e = np.stack(e)
    return e, quads(b, e)
def big(v):
    v = v.astype(np.float32)
    v[np.abs(v) < np.float32(2.0 ** -16)] = 0
    return v.astype(BF)
def coarse(v):
    v = v.copy()
    v[:, N:] = 0
    return np.stack([v.reshape(128, 512)] * N)
def planted(rng, cell, low=False):
    at = rng.permutation(N)[np.arange(128) // (128 // N)]
    c = (1 + rng.random((128, 128, 4))) * (at[:, None] == np.arange(128)[None, :])[:, :, None]
    on = at[None, :, None] == cell[:, None, :]
    v = np.where(on[:, :, :, None], 8 + 8 * rng.random((N, 128, T, 4)), 2 * rng.random((N, 128, T, 4)) - 1)
    if low:
        u = 1 + rng.random((N, 128, T // 2, 4))
        v[:, :, 1::2] = np.where(on[:, :, 1::2, None], -0.5 * u, -8 * u)
        c = c * 2.0 ** 20
    v = v * np.exp2(rng.integers(-3, 4, (N, 1, T, 1)))
    return {"x": big(v.reshape(N, 128, 4 * T)), "co": coarse(big(c))}
def setup_inputs(rng):
    return {"x": big(f(rng, N, 128, 4 * T)), "co": coarse(big(f(rng, 128, 512)).reshape(128, 128, 4)), "b1": big(f(rng, N, 128, 512)), "b2": big(f(rng, N, 128, 512)), "w": f(rng, N, 128, 512)}
def setup_inputs_spread(rng):
    d = setup_inputs(rng)
    d["x"], d["b1"] = big(wide(rng, N, 128, 4 * T, cols=6)), big(wide(rng, N, 128, 512))
    return d
def setup_inputs_ties(rng):
    d = setup_inputs(rng)
    for k in ("b1", "b2"):
        b = d[k].reshape(N, 128, 128, 4).copy()
        for r in range(N):
            for h in range(4): b[r, 32 * h:32 * h + 32] = b[r, 32 * h:32 * h + 32][:, rng.permutation(128) % 32]
        d[k] = b.reshape(N, 128, 512)
    c = d["co"][0].reshape(128, 128, 4).copy()
    c[:, :N] = c[:, rng.permutation(N) % (N // 2)]
    d["co"] = coarse(c)
    return d
def setup_inputs_crowd(rng):
    g, cell = int(rng.integers(0, N)), []
    for s in range(N):
        o = rng.permutation(np.delete(np.arange(N), g))
        if o[0] == s: o = o[::-1]
        m = int(rng.integers(1, 17))
        cell.append(rng.permutation(np.concatenate([np.full(CAPP + m, g), np.full(CAPP, o[0]), o[1:][rng.integers(0, N - 2, T - 2 * CAPP - m)]])))
    return {**setup_inputs(rng), **planted(rng, np.stack(cell))}
def setup_inputs_few(rng):
    g, a, b = [int(i) for i in rng.permutation(N)[:3]]
    cell = np.delete(np.arange(N), g)[rng.integers(0, N - 1, (N, T))]
    cell[a], cell[b] = a, a
    return {**setup_inputs(rng), **planted(rng, cell, low=True)}
def setup_inputs_zero(rng):
    d, h = setup_inputs(rng), [int(i) for i in rng.permutation(4)]
    neg, pat, gap = [slice(32 * i, 32 * i + 32) for i in h[:3]]
    p = (1 + rng.random((32, 1, 4))) * np.exp2(rng.integers(-2, 3, (32, 1, 1)))
    v, b, c = d["x"].astype(np.float32).reshape(N, 128, T, 4), d["b1"].astype(np.float32).reshape(N, 128, 128, 4), d["co"][0].reshape(128, 128, 4).copy()
    u = d["b2"].astype(np.float32)
    c[neg], c[pat] = 0, 0
    c[:, int(rng.integers(0, N))] = 0
    v[:, neg], b[:, neg], u[:, neg] = -np.abs(v[:, neg]), np.abs(b[:, neg]), np.abs(u[:, neg])
    v[:, pat] = p
    for r in range(N):
        e, k = rng.permutation(T), rng.integers(0, 4, 128)
        v[r, gap][:, e[T // 8:T // 2]] = 0
        v[r][:, e[:T // 8]] = 0
        k[int(rng.integers(0, 128))] = 0
        b[r, pat] = p * np.exp2(-k.astype(np.float64))[:, None]
        if r % 2 == 0: b[r, neg, int(rng.integers(0, 128))] = 0
    k = np.float32(2.0 ** 20)
    d["x"], d["b1"], d["b2"], d["co"] = big(v.reshape(N, 128, 4 * T) * k), big(b.reshape(N, 128, 512) * k), big(u * k), coarse(c)
    return d
def check_inputs(d):
    b = []
    for k in ("x", "co", "b1", "b2", "w"):
        v = np.abs(d[k].astype(np.float32))
        if not (np.isfinite(v).all() and ((v == 0) | (v >= 2.0 ** -30) & (v <= 2.0 ** 30)).all()): b.append("a value of " + k)
    c = d["co"].astype(np.float32)
    if (c[:, :, 4 * N:] != 0).any(): b.append("co has numbers behind its first N columns")
    if (c != c[:1]).any(): b.append("co isn't the same on all ranks")
    return b
def reference(x, co, b1, b2, w):
    oc, osc = np.zeros((N, 128, 8 * T), np.uint8), np.zeros((N, 16, 2 * T), np.uint8)
    wn, y = np.full((N, 8, T), -1, np.float32), np.zeros((N, 128, T), np.float32)
    q = [mx_ref.quantize(x[s]) for s in range(N)]
    taken = np.full((N, N, CAPP), -1)
    for s in range(N):
        cell = np.argmax(mx_ref.matmul(mx_ref.quantize(co[s]), q[s])[:N] + np.float32(0), axis=0)
        for d in range(N):
            t = np.flatnonzero(cell == d)[:CAPP]
            taken[s, d, :len(t)] = t
    home = [pick(q[s], np.full(2 * T, -1)) for s in range(N)]
    for d in range(N):
        z = join(*[pick(q[s], taken[s, d]) for s in range(N)])
        n1, v1 = level(mx_ref.quantize(b1[d]), z)
        r = mx_ref.quantize((decode(z) - decode(v1)).astype(BF))
        n2, v2 = level(mx_ref.quantize(b2[d]), r)
        for s in range(N):
            k = np.flatnonzero(taken[s, d] >= 0)
            t, i = taken[s, d][k], s * CAPP + k
            wn[s, :4, t], wn[s, 4:, t] = n1[:, i].T, n2[:, i].T
            home[s] = put(put(home[s], t, pick(v1, i)), T + t, pick(v2, i))
    for s in range(N):
        oc[s], osc[s] = emit(home[s])
        m = mx_ref.matmul(mx_ref.quantize(w[s]), home[s])
        y[s] = m[:, :T] + m[:, T:]
    return {"oc": oc, "osc": osc, "wn": wn, "y": y}

@@ -1,0 +1,348 @@
+from concourse.bass import DstId, RemoteDMATransfer
+from concourse.mybir import dt, AluOpType, AxisListType, ActivationFunctionType
+
+BF, F32, I32, U16, COD, PL = "bfloat16", "float32", "int32", "uint16", "float8_e4m3fn_x4", "uint8"
+SCRATCH = {
+    "xt": ("sbuf", [128, 512], BF), "cot": ("sbuf", [128, 512], BF), "wt": ("sbuf", [128, 512], BF),
+    "br1": ("sbuf", [128, 512], BF), "br2": ("sbuf", [128, 512], BF), "bt1": ("sbuf", [128, 2048], BF), "bt2": ("sbuf", [128, 2048], BF),
+    "et": ("sbuf", [128, 2048], BF), "en": ("sbuf", [128, 1536], BF), "st": ("sbuf", [128, 512], BF),
+    "trt": ("sbuf", [128, 512], BF), "ct": ("sbuf", [128, 512], BF), "mt": ("sbuf", [128, 512], BF),
+    "rqt": ("sbuf", [128, 576], BF), "ht": ("sbuf", [128, 512], BF), "zt": ("sbuf", [128, 512], BF),
+    "rt": ("sbuf", [128, 1024], BF),
+    "jd": ("sbuf", [128, 128], BF), "dg": ("sbuf", [128, 128], BF), "tri": ("sbuf", [128, 128], BF),
+    "low": ("sbuf", [128, 8], F32), "rs": ("sbuf", [128, 256], F32), "ri0": ("sbuf", [128, 32], BF), "ri": ("sbuf", [128, 256], BF),
+    "qrow": ("sbuf", [128, 16], F32), "nrow": ("sbuf", [128, 16], F32), "crow": ("sbuf", [128, 8], F32), "qm4": ("sbuf", [128, 4], F32),
+    "pm": ("sbuf", [128, 4], F32), "ph": ("sbuf", [128, 4], F32), "pl": ("sbuf", [128, 4], F32), "pr": ("sbuf", [128, 4], F32), "pq": ("sbuf", [128, 4], F32),
+    "lo75": ("sbuf", [128, 4], F32), "qoff": ("sbuf", [128, 4], F32), "mask8": ("sbuf", [128, 8], F32),
+    "rmc": ("sbuf", [128, 8], F32), "val": ("sbuf", [128, 4], F32), "s16": ("sbuf", [128, 4], F32),
+    "qone": ("sbuf", [128, 16], F32), "qa": ("sbuf", [128, 16], F32), "qj": ("sbuf", [128, 16], F32), "qk": ("sbuf", [128, 16], F32),
+    "ha": ("sbuf", [128, 4], F32), "hb": ("sbuf", [128, 4], F32),
+    "hk": ("sbuf", [128, 4], F32), "hr": ("sbuf", [128, 4], F32), "hrr": ("sbuf", [128, 4], F32),
+    "loff": ("sbuf", [128, 16], U16), "hoff": ("sbuf", [128, 8], U16),
+    "rm1": ("sbuf", [128, 1024], F32), "rm2": ("sbuf", [128, 1024], F32), "sg1": ("sbuf", [128, 1024], BF), "sg2": ("sbuf", [128, 1024], BF),
+    "n1": ("sbuf", [128, 8], F32), "n2": ("sbuf", [128, 8], F32), "m1": ("sbuf", [128, 32], BF), "m2": ("sbuf", [128, 32], BF),
+    "td1": ("sbuf", [128, 64], BF), "td2": ("sbuf", [128, 64], BF),
+    "tt1": ("sbuf", [128, 64], BF), "tt2": ("sbuf", [128, 64], BF), "off1": ("sbuf", [128, 16], U16), "off2": ("sbuf", [128, 16], U16),
+    "ws1": ("dram", [8, 128, 1], BF), "wl1": ("dram", [8, 128, 1], BF), "wl2": ("dram", [8, 128, 1], BF),
+    "wrow": ("sbuf", [128, 272], BF), "wnf": ("sbuf", [128, 128], F32), "yt": ("sbuf", [128, 128], F32),
+}
+for _n, _w in (("x", 128), ("co", 128), ("w", 128), ("b1", 512), ("b2", 512), ("e", 512), ("ne", 384), ("st", 128), ("n3", 128), ("tr", 128), ("c", 128),
+               ("m", 128), ("rq", 144), ("h", 128), ("slot", 256), ("land", 256), ("va", 256), ("r", 256), ("vb", 256),
+               ("hva", 272), ("hvb", 272), ("oa", 128), ("ob", 128)):
+    SCRATCH["k_" + _n] = ("sbuf", [128, _w], COD)
+    SCRATCH["s_" + _n] = ("sbuf", [128, _w], PL)
+for _n in range(8):
+    SCRATCH["p%d" % _n] = ("psum", [128, 512], F32)
+SEMAPHORES = ["cv", "cs", "ce", "cg", "dx", "dco", "db1", "db2", "dw", "dn1", "do1", "do2", "df1", "df2", "dst", "dso",
+              "ra", "rb", "rva", "rvb", "rn1", "rn2", "rs", "dn3", "dz", "loc"]
+
+ADD, SUB, MUL, MAX = AluOpType.add, AluOpType.subtract, AluOpType.mult, AluOpType.max
+MIN, GE, EQ, NE = AluOpType.min, AluOpType.is_ge, AluOpType.is_equal, AluOpType.not_equal
+COPY, SIGN = ActivationFunctionType.Copy, ActivationFunctionType.Sign
+LOW = -1e29
+BIG = 1e29
+R16, R32 = 1.5 * 2.0 ** 27, 1.5 * 2.0 ** 28
+
+
+def rank_program(g, core, T, topo):
+    me = T.rank_of(core)
+    if me is None:
+        return
+    ops, queue = [], {"v": g.vector, "s": g.scalar, "e": g.tensor, "g": g, "y": g.sync}
+    own_sem = {"v": "cv", "s": "cs", "e": "ce", "g": "cg"}
+
+    def add(q, fn, deps=(), sem=None, inc=1):
+        ops.append((q, fn, list(deps), own_sem[q] if sem is None else sem, inc))
+        return len(ops) - 1
+
+    def V(fn, *deps): return add("v", fn, deps)
+    def S(fn, *deps): return add("s", fn, deps)
+    def E(fn, *deps): return add("e", fn, deps)
+    def G(fn, *deps): return add("g", fn, deps)
+    def D(q, sem, out, in_, *deps): return add(q, lambda: queue[q].dma_start(out, in_), deps, sem, 16)
+
+    v, sc, te = g.vector, g.scalar, g.tensor
+    K = lambda n, a, b: T["k_" + n][:, a:b]
+    P = lambda n, a, b: T["s_" + n][:, a:b]
+
+    def ts(out, in0, s1, s2, op0, op1, *deps):
+        return V(lambda: v.tensor_scalar(out, in0, s1, s2, op0) if op1 is None else v.tensor_scalar(out, in0, s1, s2, op0, op1), *deps)
+
+    def cp(out, in_, *deps): return V(lambda: v.tensor_copy(out, in_), *deps)
+
+    def act(out, in_, *deps): return S(lambda: sc.activation(out, in_, COPY), *deps)
+
+    def fill(ap, c): return V(lambda: v.memset(ap, c))
+
+    def quant(n, tile, a, b, src, *deps):
+        return V(lambda: v.quantize_mx(K(n, a, b), P(n, a, b), T[tile][:, src:src + 4 * (b - a)]), *deps)
+
+    def mm(bank, n, w, wa, x, xa, start, stop, *deps):
+        return E(lambda: te.matmul_mx(T["p%d" % bank][:, 0:n], K(w, wa, wa + 128), P(w, wa, wa + 128), K(x, xa, xa + n), P(x, xa, xa + n), start, stop), *deps)
+
+    def pick(o, a, b, w, wn, off, c, *deps):
+        k = (b - a) // 16
+        return (V(lambda: v.tensor_copy(K(o, a, b).bitcast(dt.uint32), K(w, 0, wn).bitcast(dt.uint32).indirect(T[off][:, c:c + k])), *deps),
+                S(lambda: sc.activation(P(o, a, b), P(w, 0, wn).indirect(T[off][:, c:c + k]), COPY), *deps))
+
+    others = [d for d in range(len(T.cores)) if d != me]
+    far = [d for d in others if topo.die(T.cores[d]) != topo.die(core)]
+    near = [d for d in others if d not in far]
+    eng = {}
+    for part, k in ((far, 0), (near, 1)):
+        for i, d in enumerate(part):
+            e = topo.engines(core, T.cores[d])[k::2]
+            w = len(e) // 4
+            eng[d] = e[w * i:w * i + w]
+    expect = {}
+
+    def send(src, dst, sem, one, *deps):
+        def call():
+            tr = []
+            for d in far + near:
+                rid, pid, _ = topo.addr(T.cores[d])
+                m = sum(1 << e for e in (eng[d][:1] if one else eng[d]))
+                tr.append(RemoteDMATransfer(dst_ids=[DstId(rid=rid, pnc=pid)], dma_engine_mask=m, remote_sem=T.sem[sem], src=src(d), dst=dst))
+            return g.remote_dma_fused(tr, local_sem=T.sem["loc"])
+        for d in others:
+            expect["loc"] = expect.get("loc", 0) + (1 if one else len(eng[d]))
+        return add("g", call, deps, "")
+
+    def arrivals(sem, ranks, n, one):
+        expect[sem] = n * sum(1 if one else len(topo.engines(T.cores[s], core)) // 8 for s in ranks if s != me)
+        return (sem, expect[sem])
+
+    dco = D("s", "dco", T.cot[:, 0:32], T.co[:, 0:32])
+    dx = D("y", "dx", T.xt[:], T.x[:])
+    db1 = D("y", "db1", T.br1[:], T.b1[:])
+    db2 = D("y", "db2", T.br2[:], T.b2[:])
+    dw = D("y", "dw", T.wt[:], T.w[:])
+
+    def affine(out, in_, step, n, op, f, base, cm, *deps): return G(lambda: g.affine_select(out, in_, [[step, n]], op, f, base, cm), *deps)
+    def iota(out, pattern, base, cm): return G(lambda: g.iota(out, pattern, base, cm, allow_small_or_imprecise_dtypes=True))
+    def smul(out, in_, c, *deps): return S(lambda: sc.activation(out, in_, COPY, scale=c), *deps)
+
+    gj = iota(T.jd[:], [[1, 128]], 0, -1)
+    gr = iota(T.ri0[:], [[2, 16], [0, 2]], -15, 0)
+    gq = iota(T.qrow[:], [[256, 8], [32, 2]], 2048, 0)
+    ztm = fill(T.zt[:], 0.0)
+    stm = fill(T.st[:], 0.0)
+    sh = ts(T.st[:, 3:64:4], T.jd[:, 16 * me:16 * me + 16], 0.0, -1.0, EQ, MUL, gj, stm)
+    qst = quant("st", "st", 0, 128, 0, sh)
+    send(lambda d: K("st", 0, 16).bitcast(dt.uint8), K("n3", 16 * me, 16 * me + 16).bitcast(dt.uint8), "rs", False, qst)
+    send(lambda d: P("st", 0, 16), P("n3", 16 * me, 16 * me + 16), "rs", False)
+
+    def neg(b): return affine(T.en[:, 512 * b:512 * b + 512], T.zt[:], 1, 512, NE, -1.0, -b, -4, ztm)
+    en = [neg(0)]
+    own3 = [D("y", "dn3", K("n3", 16 * me, 16 * me + 16).bitcast(dt.uint8), K("st", 0, 16).bitcast(dt.uint8), qst),
+            D("y", "dn3", P("n3", 16 * me, 16 * me + 16), P("st", 0, 16), qst)]
+    dg = ts(T.dg[:], T.jd[:], 0.0, 2048.0, EQ, MUL, gj)
+    tri = ts(T.tri[:], T.jd[:], 0.0, 2.0, GE, MUL)
+    tr1s = fill(T.trt[:, 1:512:2], 1.0)
+    t0 = V(lambda: v.tensor_tensor(T.trt[:, 0:512:4], T.dg[:], T.tri[:], MAX), dg, tri)
+    low = fill(T.low[:], LOW)
+
+    coz = act(T.cot[:, 32:512], T.zt[:, 0:480], ztm)
+    rr = [act(T.ri[:, 0:32], T.ri0[:], gr)]
+    for n in (32, 64, 128):
+        rr.append((lambda n: act(T.ri[:, n:2 * n], T.ri[:, 0:n], rr[-1]))(n))
+    t2 = smul(T.trt[:, 2:512:4], T.trt[:, 0:512:4], -1.0, t0)
+    mtz = act(T.mt[:], T.zt[:])
+    rqz = act(T.rqt[:, 1:576:2], T.zt[:, 0:288])
+    ez = [act(T.et[:, 512 * b:512 * b + 512], T.zt[:]) for b in range(4)]
+
+    qco = quant("co", "cot", 0, 128, 0, dco, coz)
+    qx = quant("x", "xt", 0, 128, 0, dx)
+    zc = [D("y", "dz", o, i, qco) for n in ("hva", "hvb") for o, i in ((K(n, 256, 272).bitcast(dt.uint8), K("co", 16, 32).bitcast(dt.uint8)), (P(n, 256, 272), P("co", 16, 32)))]
+    ms = mm(0, 128, "x", 0, "co", 0, True, True, qco, qx)
+    qtr = quant("tr", "trt", 0, 128, 0, t0, tr1s, t2)
+    m1c = ts(T.mt[0:1, 1:32:4], T.qrow[0:1, 0:16:2], -2048.0, None, ADD, None, gq, mtz)
+    m3c = fill(T.mt[32:33, 3:32:4], -15.0)
+    rmc = V(lambda: v.tensor_tensor_scan(T.rmc[:], T.low[:], T.p0[:, 0:8], LOW, MAX, MAX), ms, low)
+    ge0 = ts(T.mt[:, 0:32:4], T.rmc[:], T.rmc[:, 7:8], None, GE, None, rmc, mtz)
+    ge1 = ts(T.mt[:, 6:32:4], T.rmc[:, 0:7], T.rmc[:, 7:8], None, GE, None, rmc)
+    qm = quant("m", "mt", 0, 128, 0, ge0, ge1, m1c, m3c)
+    mr = mm(1, 128, "tr", 0, "m", 0, True, True, qm, qtr)
+    hi16, lo, val16, s16a = T.ph[:, 0:1], T.pl[:, 0:1], T.val[:, 0:1], T.s16[:, 0:1]
+    pm = ts(T.pm[:, 0:1], T.jd[:, 0:1], -1.0, -7.5, MUL, ADD)
+    pr = ts(T.pr[:, 0:1], T.jd[:, 0:1], -1.0, -15.5, MUL, ADD)
+    ph = ts(hi16, T.pm[:, 0:1], R16, R16, ADD, SUB, pm)
+    pq = ts(T.pq[:, 0:1], T.pr[:, 0:1], R32, R32, ADD, SUB, pr)
+    pl = ts(lo, T.pm[:, 0:1], hi16, 7.5, SUB, ADD, ph)
+    val = V(lambda: v.tensor_reduce(val16, T.p1[:, 0:8], AxisListType.X, MAX), mr)
+    s16 = ts(s16a, val16, R32, R32, ADD, SUB, val)
+    r0 = ts(T.rqt[:, 0:512:2], T.ri[:], s16a, val16, ADD, EQ, s16, rr[-1], rqz)
+    q0 = ts(T.rqt[:, 512:576:4], T.qrow[:], s16a, hi16, EQ, MUL, gq, ph)
+    q1 = ts(T.rqt[:, 514:576:4], T.qrow[:], s16a, lo, EQ, MUL, pl)
+    qrq = quant("rq", "rqt", 0, 144, 0, r0, q0, q1)
+    ml = mm(6, 128, "rq", 0, "rq", 16, True, True, qrq)
+    qsel = [ts(T.qm4[:, h:h + 1], T.pq[:, 0:1], 32.0 * h, None, EQ, None, pq) for h in range(4)]
+    loff = cp(T.loff[:], T.p6[:, 112:128], ml)
+    sk, ss = pick("slot", 0, 256, "x", 128, "loff", 0, loff)
+    send(lambda d: K("slot", 32 * d, 32 * d + 32).bitcast(dt.uint8), K("land", 32 * me, 32 * me + 32).bitcast(dt.uint8), "ra" if me < 4 else "rb", False, sk)
+    send(lambda d: P("slot", 32 * d, 32 * d + 32), P("land", 32 * me, 32 * me + 32), "ra" if me < 4 else "rb", False, ss)
+    lk, ls = pick("land", 32 * me, 32 * me + 32, "x", 128, "loff", 2 * me, loff)
+    ed = [smul(T.et[:, 512 * b + b:512 * b + 512:4], T.dg[:], 2.0 ** -11, dg, ez[b]) for b in range(4)]
+    en += [neg(b) for b in (1, 2)]
+    gn = iota(T.nrow[:], [[1, 16]], -16, 0)
+    gc = iota(T.crow[:], [[16, 8]], 0, 0)
+    htm = iota(T.ht[:], [[0, 512]], 0, 0)
+    h1 = ts(T.qone[:], T.qrow[:], s16a, None, EQ, None, s16)
+    h5 = ts(T.hr[:, 0:1], val16, s16a, 15.0, SUB, ADD, s16)
+
+    def books(i, load, onv):
+        o = []
+        for h in range(4):
+            t, r, m = T["bt%d" % i][:, 512 * h:512 * h + 512], T["br%d" % i][:], T.qm4[:, h:h + 1]
+            if h < onv:
+                o.append(ts(t, r, m, None, MUL, None, qsel[h], load))
+            else:
+                o.append(smul(t, r, m, qsel[h], load))
+        return o
+    bk1 = books(1, db1, 2)
+    qoff = ts(T.qoff[:, 0:1], T.pq[:, 0:1], 4.0, None, MUL, None, pq)
+    rs0 = fill(T.rs[:], BIG)
+    mz = [fill(T[n][:], 0.0) for n in ("m1", "m2")]
+    qe = quant("e", "et", 0, 512, 0, *ed)
+    rs = V(lambda: v.memset(T.rs[:, 0:256:128], LOW), rs0)
+    qb1 = quant("b1", "bt1", 0, 512, 0, *bk1)
+    bk2 = books(2, db2, 1)
+    qne = [quant("ne", "en", 0, 256, 0, en[0], en[1]), quant("ne", "en", 256, 384, 1024, en[2])]
+
+    def level(lev, z, book, banks, zdeps, bdeps, between, behind):
+        L = str(lev)
+        n, m, td, tt, off, rm, sg = ["%s%s" % (a, L) for a in ("n", "m", "td", "tt", "off", "rm", "sg")]
+        mmx = {(i, j): mm(banks[2 * i + j], 256, z, 128 * i, book, 256 * j, True, True, bdeps[j], *zdeps[i]) for i in (0, 1) for j in (0, 1)}
+        between()
+        scan, sign = {}, {}
+        for i in (0, 1):
+            for j in (0, 1):
+                b = "p%d" % banks[2 * i + j]
+                for o, w in (((0, 128), (128, 128)) if i == 0 and j == 0 else ((0, 256),)):
+                    c = 512 * i + 256 * j + o
+                    h = V((lambda c, b, o, w: lambda: v.tensor_tensor_scan(T[rm][:, c:c + w], T.rs[:, 0:w], T[b][:, o:o + w], LOW, MIN, MAX))(c, b, o, w), mmx[i, j], rs)
+                    for k in range(o // 128, (o + w) // 128):
+                        scan[i, 2 * j + k] = h
+        for i in (0, 1):
+            for h in range(4):
+                c = 512 * i + 128 * h
+                sign[i, h] = S((lambda i, h, c: lambda: sc.activation(T[sg][:, c:c + 128], T[rm][:, c:c + 128], SIGN, bias=T[rm][:, c + 127:c + 128], scale=-1.0, accum_out=T[n][:, 2 * h + i:2 * h + i + 1]))(i, h, c), scan[i, h])
+        mv = []
+        for h in range(4):
+            for a in range(4):
+                o, w, dep = T[m][32 * h:32 * h + 32, a:8:4], T[n][32 * a:32 * a + 32, 2 * h:2 * h + 2], (sign[0, h], sign[1, h], mz[lev - 1])
+                mv.append((cp if 4 * h + a < NV else act)(o, w, *dep))
+        behind()
+        tr = V(lambda: v.transpose(T[td][:, 16:48], T[m][:]), *mv)
+        dup = [cp(T[td][:, 0:16], T[td][:, 16:32], tr), cp(T[td][:, 48:64], T[td][:, 32:48], tr)]
+        tr2 = V(lambda: v.transpose(T[tt][:], T[td][:]), *dup)
+        of = [ts(T[off][:, a:16:2], T[tt][:, 32 * a:32 * a + 8], T.qoff[:, 0:1], None, ADD, None, tr2, qoff) for a in (0, 1)]
+        do = [D("y", "do" + L, T["wl" + L][me:me + 1, 32 * h:32 * h + 32, 0], T[td][32 * h + me:32 * h + me + 1, 16:48], tr) for h in range(4)]
+        return scan, of, mv, tr, do
+
+    NV = 11
+    arr = [arrivals("ra", range(0, 4), 2, False), arrivals("rb", range(4, 8), 2, False)]
+    zd = [[arr[i]] + ([lk, ls] if me // 4 == i else []) for i in (0, 1)]
+    bank, late = {}, {}
+    ha, hb, hk, hr, hrr = T.ha[:, 0:1], T.hb[:, 0:1], T.hk[:, 0:1], T.hr[:, 0:1], T.hrr[:, 0:1]
+
+    def behind1():
+        mk = ts(T.mask8[:], T.crow[:], hi16, None, EQ, None, ph, gc)
+        h2 = V(lambda: v.tensor_tensor(T.qa[:], T.qone[:], T.nrow[:], MUL), h1, gn)
+        h4 = S(lambda: sc.activation(T.qj[:], T.qone[:], COPY, accum_out=hk), h1)
+        h3 = S(lambda: sc.activation(T.qk[:], T.qa[:], COPY, accum_out=ha), h2)
+        h6 = S(lambda: sc.activation(hrr, hr, COPY, scale=hk), h5, h4)
+        h7 = S(lambda: sc.activation(hb, ha, COPY, bias=16.0), h3)
+        late["h"] = [S(lambda: sc.activation(T.ht[:, 1:32:4], T.mask8[:], COPY, scale=hrr), h6, mk, htm),
+                     S(lambda: sc.activation(T.ht[:, 0:32:4], T.mask8[:], COPY, scale=hb), h7, mk, htm)]
+
+    def unpack():
+        for b in range(4):
+            bank[0, b] = (2 + b, mm(2 + b, 128, "e", 128 * b, "land", 0, True, False, qe, *zd[0]))
+    scan1, of1, mv1, tr1, do1 = level(1, "land", "b1", (0, 1, 6, 7), zd, (qb1, qb1), unpack, behind1)
+    for b in range(4):
+        n = (0, 1, 6, 7)[b]
+        bank[1, b] = (n, mm(n, 128, "e", 128 * b, "land", 128, True, False, *[scan1[b // 2, 2 * (b % 2) + h] for h in (0, 1)]))
+    dn1 = [D("y", "dn1", T.ws1[:, 32 * h:32 * h + 32, 0], T.td1[32 * h:32 * h + 8, 16:48], tr1) for h in range(4)]
+    va = [pick("va", 128 * i, 128 * i + 128, "b1", 512, "off1", 8 * i, *of1) for i in (0, 1)]
+    send(lambda d: K("va", 32 * d, 32 * d + 32).bitcast(dt.uint8), K("hva", 32 * me, 32 * me + 32).bitcast(dt.uint8), "rva", False, va[0][0], va[1][0])
+    send(lambda d: P("va", 32 * d, 32 * d + 32), P("hva", 32 * me, 32 * me + 32), "rva", False, va[0][1], va[1][1])
+    send(lambda d: T.ws1[d], T.wl1[me], "rn1", True, *dn1)
+    ctm = iota(T.ct[:], [[0, 512]], 0, 0)
+    qr, rc = [], {}
+    third = arrivals("rs", range(8), 2, False)
+
+    def book2(k): return quant("b2", "bt2", 256 * k, 256 * k + 256, 1024 * k, *bk2[2 * k:2 * k + 2])
+    qb2 = [book2(0)]
+    for i in (0, 1):
+        fin = [mm(bank[i, b][0], 128, *(("ne", 128 * b) if b < 3 else ("n3", 0)), "va", 128 * i, False, True, qne[b // 2] if b < 3 else qne[1], *(va[i] + ((third, own3[0], own3[1]) if b == 3 else ()))) for b in range(4)]
+        for b in range(4):
+            rc[i, b] = (cp if b % 2 == 0 else act)(T.rt[:, 512 * i + b:512 * i + 512:4], T["p%d" % bank[i, b][0]][:, 0:128], fin[b])
+        qr.append(quant("r", "rt", 128 * i, 128 * i + 128, 512 * i, *[rc[i, b] for b in range(4)]))
+        if i == 0:
+            qb2.append(book2(1))
+
+    def behind2():
+        late["wr"] = S(lambda: sc.activation(T.wrow[:], T.zt[:, 0:272], COPY, bias=-1.0))
+    scan2, of2, mv2, tr2, do2 = level(2, "r", "b2", (2, 3, 4, 5), [[qr[0]], [qr[1]]], qb2, lambda: None, behind2)
+    send(lambda d: T.m2[:, d:d + 1], T.wl2[me], "rn2", False, *mv2)
+    vb = [pick("vb", 128 * i, 128 * i + 128, "b2", 512, "off2", 8 * i, *of2) for i in (0, 1)]
+    send(lambda d: K("vb", 32 * d, 32 * d + 32).bitcast(dt.uint8), K("hvb", 32 * me, 32 * me + 32).bitcast(dt.uint8), "rvb", False, vb[0][0], vb[1][0])
+    send(lambda d: P("vb", 32 * d, 32 * d + 32), P("hvb", 32 * me, 32 * me + 32), "rvb", False, vb[0][1], vb[1][1])
+
+    fl = [D("y", "df%d" % i, T.wrow[4 * i - 4 + h:4 * i - 3 + h, 0:256], T["wl%d" % i][:, 32 * h:32 * h + 32, 0], arrivals("rn%d" % i, range(8), 1, i == 1), late["wr"], *do)
+          for i, do in ((1, do1), (2, do2)) for h in range(4)]
+    l75 = S(lambda: sc.activation(T.lo75[:, 0:1], lo, COPY, bias=-15.0, scale=2.0), pl)
+    c0 = ts(T.ct[:, 0:512:4], T.ri[:, 0:256:2], T.lo75[:, 0:1], 16.0, EQ, MUL, l75, ctm, rr[-1])
+    c1 = ts(T.ct[:, 1:512:4], T.ri[:, 0:256:2], T.lo75[:, 0:1], 0.5, EQ, MUL, l75)
+    qh = quant("h", "ht", 0, 128, 0, *late["h"])
+    qc = quant("c", "ct", 0, 128, 0, c0, c1)
+    mh = mm(5, 128, "c", 0, "h", 0, True, True, qc, qh, scan2[1, 2], scan2[1, 3])
+    qw = quant("w", "wt", 0, 128, 0, dw)
+    ka, sa = pick("hva", 32 * me, 32 * me + 32, "b1", 512, "off1", 2 * me, *of1)
+    kb, sb = pick("hvb", 32 * me, 32 * me + 32, "b2", 512, "off2", 2 * me, *of2)
+    hoff = cp(T.hoff[:], T.p5[:, 0:8], mh)
+
+    oa = pick("oa", 0, 128, "hva", 272, "hoff", 0, hoff, zc[0], zc[1], ka, sa, arrivals("rva", range(8), 2, False))
+    y1 = mm(4, 128, "w", 0, "oa", 0, True, False, qw, scan2[1, 0], scan2[1, 1], *oa)
+    D("y", "dst", T.oc[:, 0:512], K("oa", 0, 128).bitcast(dt.uint8), oa[0])
+    for k in range(4):
+        D("y", "dst", T.osc[4 * k:4 * k + 4, 0:128], T.s_oa[32 * k:32 * k + 4, :], oa[1])
+    ob = pick("ob", 0, 128, "hvb", 272, "hoff", 0, hoff, zc[2], zc[3], kb, sb, arrivals("rvb", range(8), 2, False))
+    y2 = mm(4, 128, "w", 0, "ob", 0, False, True, *ob)
+    wn = act(T.wnf[:], T.wrow[:].indirect(T.hoff[:]), hoff, *fl)
+    D("y", "dst", T.oc[:, 512:1024], K("ob", 0, 128).bitcast(dt.uint8), ob[0])
+    for k in range(4):
+        D("y", "dst", T.osc[4 * k:4 * k + 4, 128:256], T.s_ob[32 * k:32 * k + 4, :], ob[1])
+    yc = cp(T.yt[:], T.p4[:, 0:128], y2)
+    D("s", "dso", T.y[:], T.yt[:], yc)
+    D("y", "dst", T.wn[:], T.wnf[0:8, :], wn)
+
+    total, at = {}, []
+    for q, fn, deps, sem, inc in ops:
+        if sem:
+            total[sem] = total.get(sem, 0) + inc
+        at.append((sem, total.get(sem, 0)))
+    total.update(expect)
+    known, most = {q: {} for q in queue}, {}
+
+    def wait(q, sem, n):
+        if known[q].get(sem, 0) < n:
+            queue[q].wait_ge(T.sem[sem], n)
+            known[q][sem] = n
+            most[sem] = max(most.get(sem, 0), n)
+    for q, fn, deps, sem, inc in ops:
+        need = {}
+        for d in deps:
+            s, n = d if isinstance(d, tuple) else at[d]
+            if s.startswith("d"):
+                n = total[s]
+            need[s] = max(need.get(s, 0), n)
+        for s in need:
+            wait(q, s, need[s])
+        ins = fn()
+        if sem:
+            ins.then_inc(T.sem[sem], inc)
+    for s in total:
+        if most.get(s, 0) < total[s]:
+            wait("g", s, total[s])

@@ -3,14 +3,14 @@ from concourse.mybir import dt, AluOpType, AxisListType, ActivationFunctionType
 
 BF, F32, I32, U16, COD, PL = "bfloat16", "float32", "int32", "uint16", "float8_e4m3fn_x4", "uint8"
 SCRATCH = {
-    "xt": ("sbuf", [128, 512], BF), "cot": ("sbuf", [128, 512], BF), "wt": ("sbuf", [128, 512], BF),
+    "xt": ("sbuf", [128, 512], BF), "wt": ("sbuf", [128, 512], BF),
     "br1": ("sbuf", [128, 512], BF), "br2": ("sbuf", [128, 512], BF), "bt1": ("sbuf", [128, 2048], BF), "bt2": ("sbuf", [128, 2048], BF),
-    "et": ("sbuf", [128, 2048], BF), "en": ("sbuf", [128, 1536], BF), "st": ("sbuf", [128, 512], BF),
-    "trt": ("sbuf", [128, 512], BF), "ct": ("sbuf", [128, 512], BF), "mt": ("sbuf", [128, 512], BF),
-    "rqt": ("sbuf", [128, 576], BF), "ht": ("sbuf", [128, 512], BF), "zt": ("sbuf", [128, 512], BF),
+    "et": ("sbuf", [128, 528], BF), "en": ("sbuf", [128, 528], BF), "st": ("sbuf", [128, 512], BF),
+    "trt": ("sbuf", [128, 512], BF), "ct": ("sbuf", [128, 512], BF),
+    "rqt": ("sbuf", [128, 576], BF), "ht": ("sbuf", [128, 512], BF), "zt": ("sbuf", [128, 592], BF),
     "rt": ("sbuf", [128, 1024], BF),
     "jd": ("sbuf", [128, 128], BF), "dg": ("sbuf", [128, 128], BF), "tri": ("sbuf", [128, 128], BF),
-    "low": ("sbuf", [128, 8], F32), "rs": ("sbuf", [128, 256], F32), "ri0": ("sbuf", [128, 32], BF), "ri": ("sbuf", [128, 256], BF),
+    "low": ("sbuf", [128, 8], F32), "rs": ("sbuf", [128, 256], BF), "ri0": ("sbuf", [128, 32], BF), "ri": ("sbuf", [128, 256], BF),
     "qrow": ("sbuf", [128, 16], F32), "nrow": ("sbuf", [128, 16], F32), "crow": ("sbuf", [128, 8], F32), "qm4": ("sbuf", [128, 4], F32),
     "pm": ("sbuf", [128, 4], F32), "ph": ("sbuf", [128, 4], F32), "pl": ("sbuf", [128, 4], F32), "pr": ("sbuf", [128, 4], F32), "pq": ("sbuf", [128, 4], F32),
     "lo75": ("sbuf", [128, 4], F32), "qoff": ("sbuf", [128, 4], F32), "mask8": ("sbuf", [128, 8], F32),
@@ -112,7 +112,7 @@ def rank_program(g, core, T, topo):
         expect[sem] = n * sum(1 if one else len(topo.engines(T.cores[s], core)) // 8 for s in ranks if s != me)
         return (sem, expect[sem])
 
-    dco = D("s", "dco", T.cot[:, 0:32], T.co[:, 0:32])
+    dco = D("s", "dco", T.zt[:, 560:592], T.co[:, 0:32])
     dx = D("y", "dx", T.xt[:], T.x[:])
     db1 = D("y", "db1", T.br1[:], T.b1[:])
     db2 = D("y", "db2", T.br2[:], T.b2[:])
@@ -125,15 +125,13 @@ def rank_program(g, core, T, topo):
     gj = iota(T.jd[:], [[1, 128]], 0, -1)
     gr = iota(T.ri0[:], [[2, 16], [0, 2]], -15, 0)
     gq = iota(T.qrow[:], [[256, 8], [32, 2]], 2048, 0)
-    ztm = fill(T.zt[:], 0.0)
+    gc = iota(T.crow[:], [[16, 8]], 0, 0)
+    ztm = fill(T.zt[:, 0:560], 0.0)
     stm = fill(T.st[:], 0.0)
     sh = ts(T.st[:, 3:64:4], T.jd[:, 16 * me:16 * me + 16], 0.0, -1.0, EQ, MUL, gj, stm)
     qst = quant("st", "st", 0, 128, 0, sh)
     send(lambda d: K("st", 0, 16).bitcast(dt.uint8), K("n3", 16 * me, 16 * me + 16).bitcast(dt.uint8), "rs", False, qst)
-    send(lambda d: P("st", 0, 16), P("n3", 16 * me, 16 * me + 16), "rs", False)
-
-    def neg(b): return affine(T.en[:, 512 * b:512 * b + 512], T.zt[:], 1, 512, NE, -1.0, -b, -4, ztm)
-    en = [neg(0)]
+    bk23 = affine(T.bt2[:, 1536:2048], T.br2[:], 0, 512, GE, 0.0, -96, 1, db2)
     own3 = [D("y", "dn3", K("n3", 16 * me, 16 * me + 16).bitcast(dt.uint8), K("st", 0, 16).bitcast(dt.uint8), qst),
             D("y", "dn3", P("n3", 16 * me, 16 * me + 16), P("st", 0, 16), qst)]
     dg = ts(T.dg[:], T.jd[:], 0.0, 2048.0, EQ, MUL, gj)
@@ -142,74 +140,75 @@ def rank_program(g, core, T, topo):
     t0 = V(lambda: v.tensor_tensor(T.trt[:, 0:512:4], T.dg[:], T.tri[:], MAX), dg, tri)
     low = fill(T.low[:], LOW)
 
-    coz = act(T.cot[:, 32:512], T.zt[:, 0:480], ztm)
+    ez = act(T.et[:], T.zt[:, 32:560], ztm)
+    rqz = act(T.rqt[:, 1:576:2], T.zt[:, 32:320])
+    ed = smul(T.et[:, 3:512:4], T.dg[:], 2.0 ** -11, dg, ez)
+    en = smul(T.en[:], T.et[:], -1.0, ed)
+    t2 = smul(T.trt[:, 2:512:4], T.trt[:, 0:512:4], -1.0, t0)
     rr = [act(T.ri[:, 0:32], T.ri0[:], gr)]
     for n in (32, 64, 128):
         rr.append((lambda n: act(T.ri[:, n:2 * n], T.ri[:, 0:n], rr[-1]))(n))
-    t2 = smul(T.trt[:, 2:512:4], T.trt[:, 0:512:4], -1.0, t0)
-    mtz = act(T.mt[:], T.zt[:])
-    rqz = act(T.rqt[:, 1:576:2], T.zt[:, 0:288])
-    ez = [act(T.et[:, 512 * b:512 * b + 512], T.zt[:]) for b in range(4)]
 
-    qco = quant("co", "cot", 0, 128, 0, dco, coz)
+    def unp(b): return quant("e", "et", 128 * b, 128 * b + 128, 3 - b, ed)
+
+    def book(i, h, load):
+        return smul(T["bt%d" % i][:, 512 * h:512 * h + 512], T["br%d" % i][:], T.qm4[:, h:h + 1], qsel, load)
+
+    hi16, lo, val16, s16a = T.ph[:, 0:1], T.pl[:, 0:1], T.val[:, 0:1], T.s16[:, 0:1]
+    qco = quant("co", "zt", 0, 128, 80, dco, ztm)
+    pr = ts(T.pr[:, 0:1], T.jd[:, 0:1], -1.0, -15.5, MUL, ADD)
     qx = quant("x", "xt", 0, 128, 0, dx)
     zc = [D("y", "dz", o, i, qco) for n in ("hva", "hvb") for o, i in ((K(n, 256, 272).bitcast(dt.uint8), K("co", 16, 32).bitcast(dt.uint8)), (P(n, 256, 272), P("co", 16, 32)))]
     ms = mm(0, 128, "x", 0, "co", 0, True, True, qco, qx)
-    qtr = quant("tr", "trt", 0, 128, 0, t0, tr1s, t2)
-    m1c = ts(T.mt[0:1, 1:32:4], T.qrow[0:1, 0:16:2], -2048.0, None, ADD, None, gq, mtz)
-    m3c = fill(T.mt[32:33, 3:32:4], -15.0)
-    rmc = V(lambda: v.tensor_tensor_scan(T.rmc[:], T.low[:], T.p0[:, 0:8], LOW, MAX, MAX), ms, low)
-    ge0 = ts(T.mt[:, 0:32:4], T.rmc[:], T.rmc[:, 7:8], None, GE, None, rmc, mtz)
-    ge1 = ts(T.mt[:, 6:32:4], T.rmc[:, 0:7], T.rmc[:, 7:8], None, GE, None, rmc)
-    qm = quant("m", "mt", 0, 128, 0, ge0, ge1, m1c, m3c)
-    mr = mm(1, 128, "tr", 0, "m", 0, True, True, qm, qtr)
-    hi16, lo, val16, s16a = T.ph[:, 0:1], T.pl[:, 0:1], T.val[:, 0:1], T.s16[:, 0:1]
-    pm = ts(T.pm[:, 0:1], T.jd[:, 0:1], -1.0, -7.5, MUL, ADD)
-    pr = ts(T.pr[:, 0:1], T.jd[:, 0:1], -1.0, -15.5, MUL, ADD)
-    ph = ts(hi16, T.pm[:, 0:1], R16, R16, ADD, SUB, pm)
+    m1c = ts(T.zt[0:1, 1:32:4], T.qrow[0:1, 0:16:2], -2048.0, None, ADD, None, gq, ztm)
+    m3c = fill(T.zt[32:33, 3:32:4], -15.0)
     pq = ts(T.pq[:, 0:1], T.pr[:, 0:1], R32, R32, ADD, SUB, pr)
-    pl = ts(lo, T.pm[:, 0:1], hi16, 7.5, SUB, ADD, ph)
+    rmc = V(lambda: v.tensor_tensor_scan(T.rmc[:], T.low[:], T.p0[:, 120:128], LOW, MAX, MAX), ms, low)
+    qsel = ts(T.qm4[:], T.crow[:, 0:8:2], T.pq[:, 0:1], None, EQ, None, pq, gc)
+    bk1 = [book(1, h, db1) for h in (0, 1, 2)]
+    ge0 = ts(T.zt[:, 0:32:4], T.rmc[:], T.rmc[:, 7:8], None, GE, None, rmc, ztm)
+    ge1 = ts(T.zt[:, 6:32:4], T.rmc[:, 0:7], T.rmc[:, 7:8], None, GE, None, rmc)
+    qtr = quant("tr", "trt", 0, 128, 0, t0, tr1s, t2)
+    qm = quant("m", "zt", 0, 128, 0, ge0, ge1, m1c, m3c)
+    mr = mm(1, 128, "tr", 0, "m", 0, True, True, qm, qtr)
+    rs0 = fill(T.rs[:], BIG)
+    pm = ts(T.pm[:, 0:1], T.jd[:, 0:1], -1.0, -7.5, MUL, ADD)
+    qoff = ts(T.qoff[:, 0:1], T.pq[:, 0:1], 4.0, None, MUL, None, pq)
     val = V(lambda: v.tensor_reduce(val16, T.p1[:, 0:8], AxisListType.X, MAX), mr)
+    ph = ts(hi16, T.pm[:, 0:1], R16, R16, ADD, SUB, pm)
     s16 = ts(s16a, val16, R32, R32, ADD, SUB, val)
+    pl = ts(lo, T.pm[:, 0:1], hi16, 7.5, SUB, ADD, ph)
     r0 = ts(T.rqt[:, 0:512:2], T.ri[:], s16a, val16, ADD, EQ, s16, rr[-1], rqz)
     q0 = ts(T.rqt[:, 512:576:4], T.qrow[:], s16a, hi16, EQ, MUL, gq, ph)
     q1 = ts(T.rqt[:, 514:576:4], T.qrow[:], s16a, lo, EQ, MUL, pl)
+    mz = [fill(T.m1[:], 0.0)]
     qrq = quant("rq", "rqt", 0, 144, 0, r0, q0, q1)
     ml = mm(6, 128, "rq", 0, "rq", 16, True, True, qrq)
-    qsel = [ts(T.qm4[:, h:h + 1], T.pq[:, 0:1], 32.0 * h, None, EQ, None, pq) for h in range(4)]
+    qe = [unp(0)]
     loff = cp(T.loff[:], T.p6[:, 112:128], ml)
+    mz.append(fill(T.m2[:], 0.0))
     sk, ss = pick("slot", 0, 256, "x", 128, "loff", 0, loff)
     send(lambda d: K("slot", 32 * d, 32 * d + 32).bitcast(dt.uint8), K("land", 32 * me, 32 * me + 32).bitcast(dt.uint8), "ra" if me < 4 else "rb", False, sk)
     send(lambda d: P("slot", 32 * d, 32 * d + 32), P("land", 32 * me, 32 * me + 32), "ra" if me < 4 else "rb", False, ss)
+    bk20 = affine(T.bt2[:, 0:512], T.br2[:], 0, 512, GE, 0.0, 31, -1, db2)
+    send(lambda d: P("st", 0, 16), P("n3", 16 * me, 16 * me + 16), "rs", False)
     lk, ls = pick("land", 32 * me, 32 * me + 32, "x", 128, "loff", 2 * me, loff)
-    ed = [smul(T.et[:, 512 * b + b:512 * b + 512:4], T.dg[:], 2.0 ** -11, dg, ez[b]) for b in range(4)]
-    en += [neg(b) for b in (1, 2)]
     gn = iota(T.nrow[:], [[1, 16]], -16, 0)
-    gc = iota(T.crow[:], [[16, 8]], 0, 0)
     htm = iota(T.ht[:], [[0, 512]], 0, 0)
-    h1 = ts(T.qone[:], T.qrow[:], s16a, None, EQ, None, s16)
-    h5 = ts(T.hr[:, 0:1], val16, s16a, 15.0, SUB, ADD, s16)
+    ctm = iota(T.ct[:], [[0, 512]], 0, 0)
 
-    def books(i, load, onv):
-        o = []
-        for h in range(4):
-            t, r, m = T["bt%d" % i][:, 512 * h:512 * h + 512], T["br%d" % i][:], T.qm4[:, h:h + 1]
-            if h < onv:
-                o.append(ts(t, r, m, None, MUL, None, qsel[h], load))
-            else:
-                o.append(smul(t, r, m, qsel[h], load))
-        return o
-    bk1 = books(1, db1, 2)
-    qoff = ts(T.qoff[:, 0:1], T.pq[:, 0:1], 4.0, None, MUL, None, pq)
-    rs0 = fill(T.rs[:], BIG)
-    mz = [fill(T[n][:], 0.0) for n in ("m1", "m2")]
-    qe = quant("e", "et", 0, 512, 0, *ed)
+    bk1.append(book(1, 3, db1))
+    bk2 = [book(2, h, db2) for h in (1, 2)]
     rs = V(lambda: v.memset(T.rs[:, 0:256:128], LOW), rs0)
+    qe += [unp(b) for b in (1, 2, 3)]
+    qne = [quant("ne", "en", 128 * b, 128 * b + 128, 3 - b, en) for b in range(2)]
     qb1 = quant("b1", "bt1", 0, 512, 0, *bk1)
-    bk2 = books(2, db2, 1)
-    qne = [quant("ne", "en", 0, 256, 0, en[0], en[1]), quant("ne", "en", 256, 384, 1024, en[2])]
+    qne.append(quant("ne", "en", 256, 384, 1, en))
+    quant("b2", "bt2", 384, 512, 1536, bk23)
+    quant("b2", "bt2", 128, 384, 512, *bk2)
+    qb2 = quant("b2", "bt2", 0, 128, 0, bk20)
 
-    def level(lev, z, book, banks, zdeps, bdeps, between, behind):
+    def level(lev, z, book, banks, zdeps, bdeps, between, behind, gap):
         L = str(lev)
         n, m, td, tt, off, rm, sg = ["%s%s" % (a, L) for a in ("n", "m", "td", "tt", "off", "rm", "sg")]
         mmx = {(i, j): mm(banks[2 * i + j], 256, z, 128 * i, book, 256 * j, True, True, bdeps[j], *zdeps[i]) for i in (0, 1) for j in (0, 1)}
@@ -234,21 +233,35 @@ def rank_program(g, core, T, topo):
                 mv.append((cp if 4 * h + a < NV else act)(o, w, *dep))
         behind()
         tr = V(lambda: v.transpose(T[td][:, 16:48], T[m][:]), *mv)
+        gap(0)
         dup = [cp(T[td][:, 0:16], T[td][:, 16:32], tr), cp(T[td][:, 48:64], T[td][:, 32:48], tr)]
+        gap(1)
         tr2 = V(lambda: v.transpose(T[tt][:], T[td][:]), *dup)
+        gap(2)
         of = [ts(T[off][:, a:16:2], T[tt][:, 32 * a:32 * a + 8], T.qoff[:, 0:1], None, ADD, None, tr2, qoff) for a in (0, 1)]
+        gap(3)
         do = [D("y", "do" + L, T["wl" + L][me:me + 1, 32 * h:32 * h + 32, 0], T[td][32 * h + me:32 * h + me + 1, 16:48], tr) for h in range(4)]
         return scan, of, mv, tr, do
 
     NV = 11
     arr = [arrivals("ra", range(0, 4), 2, False), arrivals("rb", range(4, 8), 2, False)]
     zd = [[arr[i]] + ([lk, ls] if me // 4 == i else []) for i in (0, 1)]
-    bank, late = {}, {}
+    bank, late = {}, {"v": [], "c": []}
     ha, hb, hk, hr, hrr = T.ha[:, 0:1], T.hb[:, 0:1], T.hk[:, 0:1], T.hr[:, 0:1], T.hrr[:, 0:1]
 
     def behind1():
-        mk = ts(T.mask8[:], T.crow[:], hi16, None, EQ, None, ph, gc)
-        h2 = V(lambda: v.tensor_tensor(T.qa[:], T.qone[:], T.nrow[:], MUL), h1, gn)
+        late["wr"] = S(lambda: sc.activation(T.wrow[:], T.zt[:, 32:304], COPY, bias=-1.0))
+        late["l75"] = S(lambda: sc.activation(T.lo75[:, 0:1], lo, COPY, bias=-15.0, scale=2.0), pl)
+
+    def gap1(k):
+        h = late["v"]
+        h.append((lambda: ts(T.qone[:], T.qrow[:], s16a, None, EQ, None, s16),
+                  lambda: ts(hr, val16, s16a, 15.0, SUB, ADD, s16),
+                  lambda: ts(T.mask8[:], T.crow[:], hi16, None, EQ, None, ph, gc),
+                  lambda: V(lambda: v.tensor_tensor(T.qa[:], T.qone[:], T.nrow[:], MUL), h[0], gn))[k]())
+
+    def behind2():
+        h1, h5, mk, h2 = late["v"]
         h4 = S(lambda: sc.activation(T.qj[:], T.qone[:], COPY, accum_out=hk), h1)
         h3 = S(lambda: sc.activation(T.qk[:], T.qa[:], COPY, accum_out=ha), h2)
         h6 = S(lambda: sc.activation(hrr, hr, COPY, scale=hk), h5, h4)
@@ -256,10 +269,14 @@ def rank_program(g, core, T, topo):
         late["h"] = [S(lambda: sc.activation(T.ht[:, 1:32:4], T.mask8[:], COPY, scale=hrr), h6, mk, htm),
                      S(lambda: sc.activation(T.ht[:, 0:32:4], T.mask8[:], COPY, scale=hb), h7, mk, htm)]
 
+    def gap2(k):
+        if k < 2:
+            late["c"].append(ts(T.ct[:, k:512:4], T.ri[:, 0:256:2], T.lo75[:, 0:1], (16.0, 0.5)[k], EQ, MUL, late["l75"], ctm, rr[-1]))
+
     def unpack():
         for b in range(4):
-            bank[0, b] = (2 + b, mm(2 + b, 128, "e", 128 * b, "land", 0, True, False, qe, *zd[0]))
-    scan1, of1, mv1, tr1, do1 = level(1, "land", "b1", (0, 1, 6, 7), zd, (qb1, qb1), unpack, behind1)
+            bank[0, b] = (2 + b, mm(2 + b, 128, "e", 128 * b, "land", 0, True, False, qe[3], *zd[0]))
+    scan1, of1, mv1, tr1, do1 = level(1, "land", "b1", (0, 1, 6, 7), zd, (qb1, qb1), unpack, behind1, gap1)
     for b in range(4):
         n = (0, 1, 6, 7)[b]
         bank[1, b] = (n, mm(n, 128, "e", 128 * b, "land", 128, True, False, *[scan1[b // 2, 2 * (b % 2) + h] for h in (0, 1)]))
@@ -268,35 +285,25 @@ def rank_program(g, core, T, topo):
     send(lambda d: K("va", 32 * d, 32 * d + 32).bitcast(dt.uint8), K("hva", 32 * me, 32 * me + 32).bitcast(dt.uint8), "rva", False, va[0][0], va[1][0])
     send(lambda d: P("va", 32 * d, 32 * d + 32), P("hva", 32 * me, 32 * me + 32), "rva", False, va[0][1], va[1][1])
     send(lambda d: T.ws1[d], T.wl1[me], "rn1", True, *dn1)
-    ctm = iota(T.ct[:], [[0, 512]], 0, 0)
     qr, rc = [], {}
     third = arrivals("rs", range(8), 2, False)
 
-    def book2(k): return quant("b2", "bt2", 256 * k, 256 * k + 256, 1024 * k, *bk2[2 * k:2 * k + 2])
-    qb2 = [book2(0)]
     for i in (0, 1):
-        fin = [mm(bank[i, b][0], 128, *(("ne", 128 * b) if b < 3 else ("n3", 0)), "va", 128 * i, False, True, qne[b // 2] if b < 3 else qne[1], *(va[i] + ((third, own3[0], own3[1]) if b == 3 else ()))) for b in range(4)]
+        fin = [mm(bank[i, b][0], 128, *(("ne", 128 * b) if b < 3 else ("n3", 0)), "va", 128 * i, False, True, qne[min(b, 2)], *(va[i] + ((third, own3[0], own3[1]) if b == 3 else ()))) for b in range(4)]
         for b in range(4):
-            rc[i, b] = (cp if b % 2 == 0 else act)(T.rt[:, 512 * i + b:512 * i + 512:4], T["p%d" % bank[i, b][0]][:, 0:128], fin[b])
+            rc[i, b] = (cp if b in ((0, 2), (2,))[i] else act)(T.rt[:, 512 * i + b:512 * i + 512:4], T["p%d" % bank[i, b][0]][:, 0:128], fin[b])
         qr.append(quant("r", "rt", 128 * i, 128 * i + 128, 512 * i, *[rc[i, b] for b in range(4)]))
-        if i == 0:
-            qb2.append(book2(1))
 
-    def behind2():
-        late["wr"] = S(lambda: sc.activation(T.wrow[:], T.zt[:, 0:272], COPY, bias=-1.0))
-    scan2, of2, mv2, tr2, do2 = level(2, "r", "b2", (2, 3, 4, 5), [[qr[0]], [qr[1]]], qb2, lambda: None, behind2)
+    scan2, of2, mv2, tr2, do2 = level(2, "r", "b2", (2, 3, 4, 5), [[qr[0]], [qr[1]]], (qb2, qb2), lambda: None, behind2, gap2)
     send(lambda d: T.m2[:, d:d + 1], T.wl2[me], "rn2", False, *mv2)
-    vb = [pick("vb", 128 * i, 128 * i + 128, "b2", 512, "off2", 8 * i, *of2) for i in (0, 1)]
-    send(lambda d: K("vb", 32 * d, 32 * d + 32).bitcast(dt.uint8), K("hvb", 32 * me, 32 * me + 32).bitcast(dt.uint8), "rvb", False, vb[0][0], vb[1][0])
-    send(lambda d: P("vb", 32 * d, 32 * d + 32), P("hvb", 32 * me, 32 * me + 32), "rvb", False, vb[0][1], vb[1][1])
+    vb = pick("vb", 0, 256, "b2", 512, "off2", 0, *of2)
+    send(lambda d: K("vb", 32 * d, 32 * d + 32).bitcast(dt.uint8), K("hvb", 32 * me, 32 * me + 32).bitcast(dt.uint8), "rvb", False, vb[0])
+    send(lambda d: P("vb", 32 * d, 32 * d + 32), P("hvb", 32 * me, 32 * me + 32), "rvb", False, vb[1])
 
     fl = [D("y", "df%d" % i, T.wrow[4 * i - 4 + h:4 * i - 3 + h, 0:256], T["wl%d" % i][:, 32 * h:32 * h + 32, 0], arrivals("rn%d" % i, range(8), 1, i == 1), late["wr"], *do)
           for i, do in ((1, do1), (2, do2)) for h in range(4)]
-    l75 = S(lambda: sc.activation(T.lo75[:, 0:1], lo, COPY, bias=-15.0, scale=2.0), pl)
-    c0 = ts(T.ct[:, 0:512:4], T.ri[:, 0:256:2], T.lo75[:, 0:1], 16.0, EQ, MUL, l75, ctm, rr[-1])
-    c1 = ts(T.ct[:, 1:512:4], T.ri[:, 0:256:2], T.lo75[:, 0:1], 0.5, EQ, MUL, l75)
     qh = quant("h", "ht", 0, 128, 0, *late["h"])
-    qc = quant("c", "ct", 0, 128, 0, c0, c1)
+    qc = quant("c", "ct", 0, 128, 0, *late["c"])
     mh = mm(5, 128, "c", 0, "h", 0, True, True, qc, qh, scan2[1, 2], scan2[1, 3])
     qw = quant("w", "wt", 0, 128, 0, dw)
     ka, sa = pick("hva", 32 * me, 32 * me + 32, "b1", 512, "off1", 2 * me, *of1)

@@ -1,47 +1,40 @@
 from concourse.bass import DstId, RemoteDMATransfer
 from concourse.mybir import dt, AluOpType, AxisListType, ActivationFunctionType
 
-BF, F32, I32, U16, COD, PL = "bfloat16", "float32", "int32", "uint16", "float8_e4m3fn_x4", "uint8"
-SCRATCH = {
-    "xt": ("sbuf", [128, 512], BF), "wt": ("sbuf", [128, 512], BF),
-    "br1": ("sbuf", [128, 512], BF), "br2": ("sbuf", [128, 512], BF), "bt1": ("sbuf", [128, 2048], BF), "bt2": ("sbuf", [128, 2048], BF),
-    "et": ("sbuf", [128, 528], BF), "en": ("sbuf", [128, 528], BF), "st": ("sbuf", [128, 512], BF),
-    "trt": ("sbuf", [128, 512], BF), "ct": ("sbuf", [128, 512], BF),
-    "rqt": ("sbuf", [128, 576], BF), "ht": ("sbuf", [128, 512], BF), "zt": ("sbuf", [128, 592], BF),
-    "rt": ("sbuf", [128, 1024], BF),
-    "jd": ("sbuf", [128, 128], BF), "dg": ("sbuf", [128, 128], BF), "tri": ("sbuf", [128, 128], BF),
-    "low": ("sbuf", [128, 8], F32), "rs": ("sbuf", [128, 256], BF), "ri0": ("sbuf", [128, 32], BF), "ri": ("sbuf", [128, 256], BF),
-    "qrow": ("sbuf", [128, 16], F32), "nrow": ("sbuf", [128, 16], F32), "crow": ("sbuf", [128, 8], F32), "qm4": ("sbuf", [128, 4], F32),
-    "pm": ("sbuf", [128, 4], F32), "ph": ("sbuf", [128, 4], F32), "pl": ("sbuf", [128, 4], F32), "pr": ("sbuf", [128, 4], F32), "pq": ("sbuf", [128, 4], F32),
-    "lo75": ("sbuf", [128, 4], F32), "qoff": ("sbuf", [128, 4], F32), "mask8": ("sbuf", [128, 8], F32),
-    "rmc": ("sbuf", [128, 8], F32), "val": ("sbuf", [128, 4], F32), "s16": ("sbuf", [128, 4], F32),
-    "qone": ("sbuf", [128, 16], F32), "qa": ("sbuf", [128, 16], F32), "qj": ("sbuf", [128, 16], F32), "qk": ("sbuf", [128, 16], F32),
-    "ha": ("sbuf", [128, 4], F32), "hb": ("sbuf", [128, 4], F32),
-    "hk": ("sbuf", [128, 4], F32), "hr": ("sbuf", [128, 4], F32), "hrr": ("sbuf", [128, 4], F32),
-    "loff": ("sbuf", [128, 16], U16), "hoff": ("sbuf", [128, 8], U16),
-    "rm1": ("sbuf", [128, 1024], F32), "rm2": ("sbuf", [128, 1024], F32), "sg1": ("sbuf", [128, 1024], BF), "sg2": ("sbuf", [128, 1024], BF),
-    "n1": ("sbuf", [128, 8], F32), "n2": ("sbuf", [128, 8], F32), "m1": ("sbuf", [128, 32], BF), "m2": ("sbuf", [128, 32], BF),
-    "td1": ("sbuf", [128, 64], BF), "td2": ("sbuf", [128, 64], BF),
-    "tt1": ("sbuf", [128, 64], BF), "tt2": ("sbuf", [128, 64], BF), "off1": ("sbuf", [128, 16], U16), "off2": ("sbuf", [128, 16], U16),
-    "ws1": ("dram", [8, 128, 1], BF), "wl1": ("dram", [8, 128, 1], BF), "wl2": ("dram", [8, 128, 1], BF),
-    "wrow": ("sbuf", [128, 272], BF), "wnf": ("sbuf", [128, 128], F32), "yt": ("sbuf", [128, 128], F32),
-}
-for _n, _w in (("x", 128), ("co", 128), ("w", 128), ("b1", 512), ("b2", 512), ("e", 512), ("ne", 384), ("st", 128), ("n3", 128), ("tr", 128), ("c", 128),
-               ("m", 128), ("rq", 144), ("h", 128), ("slot", 256), ("land", 256), ("va", 256), ("r", 256), ("vb", 256),
-               ("hva", 272), ("hvb", 272), ("oa", 128), ("ob", 128)):
+BF, F32, U16, COD, PL = "bfloat16", "float32", "uint16", "float8_e4m3fn_x4", "uint8"
+SCRATCH = {}
+for _n, _w in (("xt", 512), ("wt", 512), ("br1", 512), ("br2", 512), ("bt1", 2048), ("bt2", 2048), ("et", 528), ("en", 640), ("trt", 512), ("rqt", 640), ("zt", 624), ("rt", 1024),
+               ("jd", 128), ("dg", 128), ("rs", 256), ("ri", 256), ("sc8", 8), ("sg1", 1024), ("sg2", 1024), ("nrow", 512), ("wr1", 288), ("wr2", 288)):
+    SCRATCH[_n] = ("sbuf", [128, _w], BF)
+for _n, _w in (("low", 8), ("pc", 4), ("crow", 4), ("qm4", 4), ("ph", 4), ("pl", 4), ("pq", 4), ("qoff", 4), ("t1", 4), ("t2", 4), ("t3", 4), ("t4", 4), ("t5", 4), ("t6", 4), ("t7", 4),
+               ("rmc", 8), ("val", 4), ("cell", 4), ("hu", 4), ("tk", 4), ("rm1", 1024), ("rm2", 1024), ("tm", 320), ("td", 320), ("wf1", 128), ("wf2", 128), ("yt", 128)):
+    SCRATCH[_n] = ("sbuf", [128, _w], F32)
+for _n, _w in (("lt", 2), ("loff", 16), ("hoff", 16), ("off1", 32), ("off2", 32), ("wl1", 16), ("wl2", 16)):
+    SCRATCH[_n] = ("sbuf", [128, _w], U16)
+for _n, _w in (("x", 128), ("co", 128), ("w", 128), ("b1", 512), ("b2", 512), ("e", 512), ("ne", 416), ("n3", 128), ("tr", 128), ("m", 128), ("rq", 160),
+               ("slot", 256), ("land", 256), ("va", 256), ("r", 256), ("vb", 256), ("hva", 288), ("hvb", 288), ("oa", 128), ("ob", 128)):
     SCRATCH["k_" + _n] = ("sbuf", [128, _w], COD)
     SCRATCH["s_" + _n] = ("sbuf", [128, _w], PL)
 for _n in range(8):
     SCRATCH["p%d" % _n] = ("psum", [128, 512], F32)
-SEMAPHORES = ["cv", "cs", "ce", "cg", "dx", "dco", "db1", "db2", "dw", "dn1", "do1", "do2", "df1", "df2", "dst", "dso",
-              "ra", "rb", "rva", "rvb", "rn1", "rn2", "rs", "dn3", "dz", "loc"]
+SEMAPHORES = ["cv", "cs", "ce", "cg", "dx", "dco", "db1", "db2", "dw", "do1", "do2", "dva", "dst", "dso",
+              "ra", "rb", "rva", "rvb", "rn1", "rn2a", "rn2b", "rs", "dn3", "dz", "loc"]
 
 ADD, SUB, MUL, MAX = AluOpType.add, AluOpType.subtract, AluOpType.mult, AluOpType.max
-MIN, GE, EQ, NE = AluOpType.min, AluOpType.is_ge, AluOpType.is_equal, AluOpType.not_equal
-COPY, SIGN = ActivationFunctionType.Copy, ActivationFunctionType.Sign
+MIN, GE, EQ, LT, NE = AluOpType.min, AluOpType.is_ge, AluOpType.is_equal, AluOpType.is_lt, AluOpType.not_equal
+COPY, SIGN, IDENT = ActivationFunctionType.Copy, ActivationFunctionType.Sign, ActivationFunctionType.Identity
 LOW = -1e29
 BIG = 1e29
-R16, R32 = 1.5 * 2.0 ** 27, 1.5 * 2.0 ** 28
+SH = 14
+MZ, M0, Z0, CO = 0, 32, 64, 592
+
+
+def R(k):
+    return 1.5 * 2.0 ** 23 * k
+
+
+PLAN = {"cA": "vsvs", "cB": "svss", "m1": "ssss", "m2": "gssg", "mv0": "vsvsvsvsvsvs", "mv1": "vvsvvsvvsvvs", "mv2": "vvsvvsvvsvvs", "mv3": "vvsvvsvvsvvs", "mv4": "vvsvvsvvsvvs"}
+ORDER = [0,11,1,6,2,3,4,5,10,30,7,29,41,42,25,24,12,13,26,14,43,31,71,8,72,46,17,27,77,44,16,23,20,54,22,78,21,18,47,80,79,28,68,81,45,83,60,84,82,33,32,86,87,85,56,88,48,89,36,58,90,50,91,38,92,254,252,93,94,61,253,95,49,98,97,96,51,55,102,59,52,66,99,57,69,37,100,101,34,64,62,35,255,103,104,105,53,106,108,129,107,109,19,128,65,114,111,112,113,132,110,123,131,117,120,130,135,121,116,169,136,115,119,170,118,153,122,134,67,156,168,143,133,171,125,124,154,146,144,155,148,147,145,126,142,140,139,141,265,138,137,127,149,150,158,157,261,151,267,160,259,152,162,15,161,173,172,159,164,165,184,186,177,188,163,166,76,176,73,75,175,266,187,74,260,174,181,185,167,180,179,190,63,178,183,258,264,263,189,182,9,193,214,215,192,196,191,216,197,218,195,204,194,217,208,219,207,201,202,198,209,199,203,205,200,223,206,224,222,210,211,262,220,212,233,232,221,213,227,226,225,239,228,229,231,230,234,240,257,241,235,236,242,272,237,256,238,243,268,269,249,245,246,270,251,247,271,281,250,39,70,248,282,40,273,244,274,277,275,276,279,278,280,283,286,285,284,289,287,291,290,293,292,294,288,295,296]
 
 
 def rank_program(g, core, T, topo):
@@ -55,6 +48,7 @@ def rank_program(g, core, T, topo):
         ops.append((q, fn, list(deps), own_sem[q] if sem is None else sem, inc))
         return len(ops) - 1
 
+    def after(h): return -1 - h
     def V(fn, *deps): return add("v", fn, deps)
     def S(fn, *deps): return add("s", fn, deps)
     def E(fn, *deps): return add("e", fn, deps)
@@ -63,16 +57,22 @@ def rank_program(g, core, T, topo):
 
     v, sc, te = g.vector, g.scalar, g.tensor
     K = lambda n, a, b: T["k_" + n][:, a:b]
+    KB = lambda n, a, b: T["k_" + n][:, a:b].bitcast(dt.uint8)
     P = lambda n, a, b: T["s_" + n][:, a:b]
+    C = lambda n: T[n][:, 0:1]
 
     def ts(out, in0, s1, s2, op0, op1, *deps):
         return V(lambda: v.tensor_scalar(out, in0, s1, s2, op0) if op1 is None else v.tensor_scalar(out, in0, s1, s2, op0, op1), *deps)
 
+    def tt(out, in0, in1, op, *deps): return V(lambda: v.tensor_tensor(out, in0, in1, op), *deps)
     def cp(out, in_, *deps): return V(lambda: v.tensor_copy(out, in_), *deps)
-
+    def turn32(out, in_, *deps): return V(lambda: v.transpose(out, in_), *deps)
     def act(out, in_, *deps): return S(lambda: sc.activation(out, in_, COPY), *deps)
-
-    def fill(ap, c): return V(lambda: v.memset(ap, c))
+    def fill(ap, c, *deps): return V(lambda: v.memset(ap, c), *deps)
+    def affine(out, in_, step, n, op, f, base, cm, *deps): return G(lambda: g.affine_select(out, in_, [[step, n]], op, f, base, cm), *deps)
+    def iota(out, pattern, base, cm): return G(lambda: g.iota(out, pattern, base, cm, allow_small_or_imprecise_dtypes=True))
+    def lin(out, in_, a, b, *deps): return S(lambda: sc.activation(out, in_, COPY if isinstance(b, float) else IDENT, bias=b, scale=a), *deps)
+    def under(out, in_, top, count, *deps): return S(lambda: sc.activation(out, in_, SIGN, bias=top, scale=-1.0, accum_out=count), *deps)
 
     def quant(n, tile, a, b, src, *deps):
         return V(lambda: v.quantize_mx(K(n, a, b), P(n, a, b), T[tile][:, src:src + 4 * (b - a)]), *deps)
@@ -85,271 +85,221 @@ def rank_program(g, core, T, topo):
         return (V(lambda: v.tensor_copy(K(o, a, b).bitcast(dt.uint32), K(w, 0, wn).bitcast(dt.uint32).indirect(T[off][:, c:c + k])), *deps),
                 S(lambda: sc.activation(P(o, a, b), P(w, 0, wn).indirect(T[off][:, c:c + k]), COPY), *deps))
 
-    others = [d for d in range(len(T.cores)) if d != me]
-    far = [d for d in others if topo.die(T.cores[d]) != topo.die(core)]
-    near = [d for d in others if d not in far]
-    eng = {}
-    for part, k in ((far, 0), (near, 1)):
-        for i, d in enumerate(part):
-            e = topo.engines(core, T.cores[d])[k::2]
-            w = len(e) // 4
-            eng[d] = e[w * i:w * i + w]
+    ranks = range(len(T.cores))
+
+    def far_of(d): return [s for s in ranks if topo.die(T.cores[s]) != topo.die(T.cores[d])]
+    def near_of(d): return [s for s in ranks if s != d and s not in far_of(d)]
+    def place(d, s): return (far_of(d) + near_of(d) + [d]).index(s)
+    far, near = far_of(me), near_of(me)
+
+    def engines(s, d, form):
+        e = topo.engines(T.cores[s], T.cores[d])
+        w = len(e) // 4
+        part = far_of(s) if d in far_of(s) else near_of(s)
+        i = part.index(d)
+        if form in ("die", "die2"):
+            if len(part) == 4:
+                return e[w * i:w * i + w]
+            return [e[a * w:b * w] for a, b in (((0, 1), (1, 2), (2, 4)) if form == "die" else ((2, 3), (0, 2), (3, 4)))][i]
+        e = e[0::2] if d in far_of(s) else e[1::2]
+        w = len(e) // 4
+        return e[w * i:] if form == "every" and i == len(part) - 1 else e[w * i:w * i + w]
     expect = {}
 
-    def send(src, dst, sem, one, *deps):
+    def send(to, form, src, dst, sem, *deps):
         def call():
             tr = []
-            for d in far + near:
+            for d in to:
                 rid, pid, _ = topo.addr(T.cores[d])
-                m = sum(1 << e for e in (eng[d][:1] if one else eng[d]))
-                tr.append(RemoteDMATransfer(dst_ids=[DstId(rid=rid, pnc=pid)], dma_engine_mask=m, remote_sem=T.sem[sem], src=src(d), dst=dst))
+                tr.append(RemoteDMATransfer(dst_ids=[DstId(rid=rid, pnc=pid)], dma_engine_mask=sum(1 << e for e in engines(me, d, form)), remote_sem=T.sem[sem], src=src(d), dst=dst(d)))
             return g.remote_dma_fused(tr, local_sem=T.sem["loc"])
-        for d in others:
-            expect["loc"] = expect.get("loc", 0) + (1 if one else len(eng[d]))
+        expect["loc"] = expect.get("loc", 0) + sum(len(engines(me, d, form)) for d in to)
         return add("g", call, deps, "")
 
-    def arrivals(sem, ranks, n, one):
-        expect[sem] = n * sum(1 if one else len(topo.engines(T.cores[s], core)) // 8 for s in ranks if s != me)
+    def arrivals(sem, *calls):
+        expect[sem] = sum(len(engines(s, me, form)) for frm, form in calls for s in frm)
         return (sem, expect[sem])
 
-    dco = D("s", "dco", T.zt[:, 560:592], T.co[:, 0:32])
+    dco = D("s", "dco", T.zt[:, CO:CO + 32], T.co[:, 0:32])
     dx = D("y", "dx", T.xt[:], T.x[:])
-    db1 = D("y", "db1", T.br1[:], T.b1[:])
-    db2 = D("y", "db2", T.br2[:], T.b2[:])
+    db = [D("y", "db1", T.br1[:], T.b1[:]), D("y", "db2", T.br2[:], T.b2[:])]
     dw = D("y", "dw", T.wt[:], T.w[:])
 
-    def affine(out, in_, step, n, op, f, base, cm, *deps): return G(lambda: g.affine_select(out, in_, [[step, n]], op, f, base, cm), *deps)
-    def iota(out, pattern, base, cm): return G(lambda: g.iota(out, pattern, base, cm, allow_small_or_imprecise_dtypes=True))
-    def smul(out, in_, c, *deps): return S(lambda: sc.activation(out, in_, COPY, scale=c), *deps)
-
     gj = iota(T.jd[:], [[1, 128]], 0, -1)
-    gr = iota(T.ri0[:], [[2, 16], [0, 2]], -15, 0)
-    gq = iota(T.qrow[:], [[256, 8], [32, 2]], 2048, 0)
-    gc = iota(T.crow[:], [[16, 8]], 0, 0)
-    ztm = fill(T.zt[:, 0:560], 0.0)
-    stm = fill(T.st[:], 0.0)
-    sh = ts(T.st[:, 3:64:4], T.jd[:, 16 * me:16 * me + 16], 0.0, -1.0, EQ, MUL, gj, stm)
-    qst = quant("st", "st", 0, 128, 0, sh)
-    send(lambda d: K("st", 0, 16).bitcast(dt.uint8), K("n3", 16 * me, 16 * me + 16).bitcast(dt.uint8), "rs", False, qst)
-    bk23 = affine(T.bt2[:, 1536:2048], T.br2[:], 0, 512, GE, 0.0, -96, 1, db2)
-    own3 = [D("y", "dn3", K("n3", 16 * me, 16 * me + 16).bitcast(dt.uint8), K("st", 0, 16).bitcast(dt.uint8), qst),
-            D("y", "dn3", P("n3", 16 * me, 16 * me + 16), P("st", 0, 16), qst)]
-    dg = ts(T.dg[:], T.jd[:], 0.0, 2048.0, EQ, MUL, gj)
-    tri = ts(T.tri[:], T.jd[:], 0.0, 2.0, GE, MUL)
-    tr1s = fill(T.trt[:, 1:512:2], 1.0)
-    t0 = V(lambda: v.tensor_tensor(T.trt[:, 0:512:4], T.dg[:], T.tri[:], MAX), dg, tri)
-    low = fill(T.low[:], LOW)
-
-    ez = act(T.et[:], T.zt[:, 32:560], ztm)
-    rqz = act(T.rqt[:, 1:576:2], T.zt[:, 32:320])
-    ed = smul(T.et[:, 3:512:4], T.dg[:], 2.0 ** -11, dg, ez)
-    en = smul(T.en[:], T.et[:], -1.0, ed)
-    t2 = smul(T.trt[:, 2:512:4], T.trt[:, 0:512:4], -1.0, t0)
-    rr = [act(T.ri[:, 0:32], T.ri0[:], gr)]
-    for n in (32, 64, 128):
-        rr.append((lambda n: act(T.ri[:, n:2 * n], T.ri[:, 0:n], rr[-1]))(n))
-
-    def unp(b): return quant("e", "et", 128 * b, 128 * b + 128, 3 - b, ed)
-
-    def book(i, h, load):
-        return smul(T["bt%d" % i][:, 512 * h:512 * h + 512], T["br%d" % i][:], T.qm4[:, h:h + 1], qsel, load)
-
-    hi16, lo, val16, s16a = T.ph[:, 0:1], T.pl[:, 0:1], T.val[:, 0:1], T.s16[:, 0:1]
-    qco = quant("co", "zt", 0, 128, 80, dco, ztm)
-    pr = ts(T.pr[:, 0:1], T.jd[:, 0:1], -1.0, -15.5, MUL, ADD)
-    qx = quant("x", "xt", 0, 128, 0, dx)
-    zc = [D("y", "dz", o, i, qco) for n in ("hva", "hvb") for o, i in ((K(n, 256, 272).bitcast(dt.uint8), K("co", 16, 32).bitcast(dt.uint8)), (P(n, 256, 272), P("co", 16, 32)))]
-    ms = mm(0, 128, "x", 0, "co", 0, True, True, qco, qx)
-    m1c = ts(T.zt[0:1, 1:32:4], T.qrow[0:1, 0:16:2], -2048.0, None, ADD, None, gq, ztm)
-    m3c = fill(T.zt[32:33, 3:32:4], -15.0)
-    pq = ts(T.pq[:, 0:1], T.pr[:, 0:1], R32, R32, ADD, SUB, pr)
-    rmc = V(lambda: v.tensor_tensor_scan(T.rmc[:], T.low[:], T.p0[:, 120:128], LOW, MAX, MAX), ms, low)
-    qsel = ts(T.qm4[:], T.crow[:, 0:8:2], T.pq[:, 0:1], None, EQ, None, pq, gc)
-    bk1 = [book(1, h, db1) for h in (0, 1, 2)]
-    ge0 = ts(T.zt[:, 0:32:4], T.rmc[:], T.rmc[:, 7:8], None, GE, None, rmc, ztm)
-    ge1 = ts(T.zt[:, 6:32:4], T.rmc[:, 0:7], T.rmc[:, 7:8], None, GE, None, rmc)
+    gp = iota(T.pc[:, 0:2], [[-16, 2]], -15, 2)
+    gc = iota(T.crow[:], [[64, 4]], 0, 0)
+    gr = iota(T.ri[:], [[0, 8], [1, 16], [16, 2]], 0, 0)
+    gn = iota(T.nrow[:], [[0, 4], [1, 128]], 0, 0)
+    enm = fill(T.en[:], 0.0)
+    ztm = fill(T.zt[:, MZ:CO], 0.0)
+    e0 = ts(T.en[:, 3:512:4], T.jd[:], 0.0, -1.0, EQ, MUL, gj, enm)
+    e1 = ts(T.en[:, 516:516 + 4 * SH:4], T.jd[:, SH * me:SH * me + SH], 0.0, -1.0, EQ, MUL, gj, enm)
+    e2 = ts(T.en[:, 516 + 4 * SH:580 + 4 * SH:4], T.jd[:, 8 * SH:128], 0.0, -1.0, EQ, MUL, gj, enm)
+    qne = [quant("ne", "en", 128 * b, 128 * b + 128, 3 - b, e0) for b in (0, 1)] + [quant("ne", "en", 256, 400 + SH, 1, e0, e1, e2)]
+    send(far + near, "every", lambda d: KB("ne", 384, 384 + SH), lambda d: KB("n3", SH * me, SH * me + SH), "rs", qne[2])
+    send(far + near, "all", lambda d: P("ne", 384, 384 + SH), lambda d: P("n3", SH * me, SH * me + SH), "rs", qne[2])
+    own3 = [D("y", "dn3", f("n3", a, a + n), f("ne", b, b + n), qne[2]) for f in (KB, P) for a, b, n in ((SH * me, 384, SH), (8 * SH, 384 + SH, 128 - 8 * SH))]
+    third = arrivals("rs", (far + near, "every"), (far + near, "all"))
+    dg = ts(T.dg[:], T.jd[:], 0.0, 256.0, EQ, MUL, gj)
+    tr1s = act(T.trt[:, 1:512:2], T.zt[:, Z0:Z0 + 256], ztm)
+    t0 = affine(T.trt[:, 0:512:4], T.dg[:], -1, 128, GE, 1.0, 0, 1, dg)
+    t2 = lin(T.trt[:, 2:512:4], T.trt[:, 0:512:4], -1.0, 0.0, t0)
     qtr = quant("tr", "trt", 0, 128, 0, t0, tr1s, t2)
-    qm = quant("m", "zt", 0, 128, 0, ge0, ge1, m1c, m3c)
-    mr = mm(1, 128, "tr", 0, "m", 0, True, True, qm, qtr)
-    rs0 = fill(T.rs[:], BIG)
-    pm = ts(T.pm[:, 0:1], T.jd[:, 0:1], -1.0, -7.5, MUL, ADD)
-    qoff = ts(T.qoff[:, 0:1], T.pq[:, 0:1], 4.0, None, MUL, None, pq)
-    val = V(lambda: v.tensor_reduce(val16, T.p1[:, 0:8], AxisListType.X, MAX), mr)
-    ph = ts(hi16, T.pm[:, 0:1], R16, R16, ADD, SUB, pm)
-    s16 = ts(s16a, val16, R32, R32, ADD, SUB, val)
-    pl = ts(lo, T.pm[:, 0:1], hi16, 7.5, SUB, ADD, ph)
-    r0 = ts(T.rqt[:, 0:512:2], T.ri[:], s16a, val16, ADD, EQ, s16, rr[-1], rqz)
-    q0 = ts(T.rqt[:, 512:576:4], T.qrow[:], s16a, hi16, EQ, MUL, gq, ph)
-    q1 = ts(T.rqt[:, 514:576:4], T.qrow[:], s16a, lo, EQ, MUL, pl)
-    mz = [fill(T.m1[:], 0.0)]
-    qrq = quant("rq", "rqt", 0, 144, 0, r0, q0, q1)
-    ml = mm(6, 128, "rq", 0, "rq", 16, True, True, qrq)
-    qe = [unp(0)]
-    loff = cp(T.loff[:], T.p6[:, 112:128], ml)
-    mz.append(fill(T.m2[:], 0.0))
-    sk, ss = pick("slot", 0, 256, "x", 128, "loff", 0, loff)
-    send(lambda d: K("slot", 32 * d, 32 * d + 32).bitcast(dt.uint8), K("land", 32 * me, 32 * me + 32).bitcast(dt.uint8), "ra" if me < 4 else "rb", False, sk)
-    send(lambda d: P("slot", 32 * d, 32 * d + 32), P("land", 32 * me, 32 * me + 32), "ra" if me < 4 else "rb", False, ss)
-    bk20 = affine(T.bt2[:, 0:512], T.br2[:], 0, 512, GE, 0.0, 31, -1, db2)
-    send(lambda d: P("st", 0, 16), P("n3", 16 * me, 16 * me + 16), "rs", False)
-    lk, ls = pick("land", 32 * me, 32 * me + 32, "x", 128, "loff", 2 * me, loff)
-    gn = iota(T.nrow[:], [[1, 16]], -16, 0)
-    htm = iota(T.ht[:], [[0, 512]], 0, 0)
-    ctm = iota(T.ct[:], [[0, 512]], 0, 0)
+    low = fill(T.low[:], LOW)
+    rqz = act(T.rqt[:, 1:640:2], T.zt[:, Z0:Z0 + 320], ztm)
+    ed = lin(T.et[:, 0:516], T.en[:, 0:516], -1.0, 0.0, e0)
+    qe = [quant("e", "et", 128 * b, 128 * b + 128, 3 - b, ed) for b in range(4)]
+    rs = fill(T.rs[:, 0:256:128], LOW, fill(T.rs[:], BIG))
+    tmz = fill(T.tm[:], 0.0)
+    wm = [fill(T["wr%d" % i][:, 0:32], -1.0) for i in (1, 2)]
+    hi2, lo2, val, q64, qo = C("ph"), C("pl"), C("val"), C("pq"), C("qoff")
+    pq = ts(q64, T.pc[:, 1:2], R(64), R(64), ADD, SUB, gp)
+    ph = ts(hi2, T.pc[:, 0:1], R(32), R(32), ADD, SUB, gp)
+    pl = ts(lo2, T.pc[:, 0:1], hi2, 15.0, SUB, ADD, ph)
+    qsel = ts(T.qm4[:], T.crow[:], q64, None, EQ, None, pq, gc)
+    qoff = lin(qo, q64, 2.0, 0.0, pq)
+    a4 = ts(C("t2"), C("t1"), R(4), R(4), ADD, SUB, lin(C("t1"), lo2, 1.0, -1.0, pl))
+    swap = ts(C("t4"), C("t3"), q64, hi2, ADD, NE, ts(C("t3"), lo2, C("t2"), 16.0, SUB, MUL, a4), pq)
+    diag = ts(C("t5"), C("t2"), 16.0, q64, MUL, EQ, a4, pq)
+    lt = ts(T.lt[:, 0:1], C("t2"), 0.25, C("t7"), MUL, ADD, lin(C("t7"), C("t5"), -4.0, C("t6"), diag, lin(C("t6"), C("t4"), 32.0, 4.0, swap)))
 
-    bk1.append(book(1, 3, db1))
-    bk2 = [book(2, h, db2) for h in (1, 2)]
-    rs = V(lambda: v.memset(T.rs[:, 0:256:128], LOW), rs0)
-    qe += [unp(b) for b in (1, 2, 3)]
-    qne = [quant("ne", "en", 128 * b, 128 * b + 128, 3 - b, en) for b in range(2)]
-    qb1 = quant("b1", "bt1", 0, 512, 0, *bk1)
-    qne.append(quant("ne", "en", 256, 384, 1, en))
-    quant("b2", "bt2", 384, 512, 1536, bk23)
-    quant("b2", "bt2", 128, 384, 512, *bk2)
-    qb2 = quant("b2", "bt2", 0, 128, 0, bk20)
-
-    def level(lev, z, book, banks, zdeps, bdeps, between, behind, gap):
-        L = str(lev)
-        n, m, td, tt, off, rm, sg = ["%s%s" % (a, L) for a in ("n", "m", "td", "tt", "off", "rm", "sg")]
-        mmx = {(i, j): mm(banks[2 * i + j], 256, z, 128 * i, book, 256 * j, True, True, bdeps[j], *zdeps[i]) for i in (0, 1) for j in (0, 1)}
-        between()
-        scan, sign = {}, {}
-        for i in (0, 1):
-            for j in (0, 1):
-                b = "p%d" % banks[2 * i + j]
-                for o, w in (((0, 128), (128, 128)) if i == 0 and j == 0 else ((0, 256),)):
-                    c = 512 * i + 256 * j + o
-                    h = V((lambda c, b, o, w: lambda: v.tensor_tensor_scan(T[rm][:, c:c + w], T.rs[:, 0:w], T[b][:, o:o + w], LOW, MIN, MAX))(c, b, o, w), mmx[i, j], rs)
-                    for k in range(o // 128, (o + w) // 128):
-                        scan[i, 2 * j + k] = h
-        for i in (0, 1):
-            for h in range(4):
-                c = 512 * i + 128 * h
-                sign[i, h] = S((lambda i, h, c: lambda: sc.activation(T[sg][:, c:c + 128], T[rm][:, c:c + 128], SIGN, bias=T[rm][:, c + 127:c + 128], scale=-1.0, accum_out=T[n][:, 2 * h + i:2 * h + i + 1]))(i, h, c), scan[i, h])
-        mv = []
-        for h in range(4):
-            for a in range(4):
-                o, w, dep = T[m][32 * h:32 * h + 32, a:8:4], T[n][32 * a:32 * a + 32, 2 * h:2 * h + 2], (sign[0, h], sign[1, h], mz[lev - 1])
-                mv.append((cp if 4 * h + a < NV else act)(o, w, *dep))
-        behind()
-        tr = V(lambda: v.transpose(T[td][:, 16:48], T[m][:]), *mv)
-        gap(0)
-        dup = [cp(T[td][:, 0:16], T[td][:, 16:32], tr), cp(T[td][:, 48:64], T[td][:, 32:48], tr)]
-        gap(1)
-        tr2 = V(lambda: v.transpose(T[tt][:], T[td][:]), *dup)
-        gap(2)
-        of = [ts(T[off][:, a:16:2], T[tt][:, 32 * a:32 * a + 8], T.qoff[:, 0:1], None, ADD, None, tr2, qoff) for a in (0, 1)]
-        gap(3)
-        do = [D("y", "do" + L, T["wl" + L][me:me + 1, 32 * h:32 * h + 32, 0], T[td][32 * h + me:32 * h + me + 1, 16:48], tr) for h in range(4)]
-        return scan, of, mv, tr, do
-
-    NV = 11
-    arr = [arrivals("ra", range(0, 4), 2, False), arrivals("rb", range(4, 8), 2, False)]
-    zd = [[arr[i]] + ([lk, ls] if me // 4 == i else []) for i in (0, 1)]
-    bank, late = {}, {"v": [], "c": []}
-    ha, hb, hk, hr, hrr = T.ha[:, 0:1], T.hb[:, 0:1], T.hk[:, 0:1], T.hr[:, 0:1], T.hrr[:, 0:1]
-
-    def behind1():
-        late["wr"] = S(lambda: sc.activation(T.wrow[:], T.zt[:, 32:304], COPY, bias=-1.0))
-        late["l75"] = S(lambda: sc.activation(T.lo75[:, 0:1], lo, COPY, bias=-15.0, scale=2.0), pl)
-
-    def gap1(k):
-        h = late["v"]
-        h.append((lambda: ts(T.qone[:], T.qrow[:], s16a, None, EQ, None, s16),
-                  lambda: ts(hr, val16, s16a, 15.0, SUB, ADD, s16),
-                  lambda: ts(T.mask8[:], T.crow[:], hi16, None, EQ, None, ph, gc),
-                  lambda: V(lambda: v.tensor_tensor(T.qa[:], T.qone[:], T.nrow[:], MUL), h[0], gn))[k]())
-
-    def behind2():
-        h1, h5, mk, h2 = late["v"]
-        h4 = S(lambda: sc.activation(T.qj[:], T.qone[:], COPY, accum_out=hk), h1)
-        h3 = S(lambda: sc.activation(T.qk[:], T.qa[:], COPY, accum_out=ha), h2)
-        h6 = S(lambda: sc.activation(hrr, hr, COPY, scale=hk), h5, h4)
-        h7 = S(lambda: sc.activation(hb, ha, COPY, bias=16.0), h3)
-        late["h"] = [S(lambda: sc.activation(T.ht[:, 1:32:4], T.mask8[:], COPY, scale=hrr), h6, mk, htm),
-                     S(lambda: sc.activation(T.ht[:, 0:32:4], T.mask8[:], COPY, scale=hb), h7, mk, htm)]
-
-    def gap2(k):
-        if k < 2:
-            late["c"].append(ts(T.ct[:, k:512:4], T.ri[:, 0:256:2], T.lo75[:, 0:1], (16.0, 0.5)[k], EQ, MUL, late["l75"], ctm, rr[-1]))
-
-    def unpack():
-        for b in range(4):
-            bank[0, b] = (2 + b, mm(2 + b, 128, "e", 128 * b, "land", 0, True, False, qe[3], *zd[0]))
-    scan1, of1, mv1, tr1, do1 = level(1, "land", "b1", (0, 1, 6, 7), zd, (qb1, qb1), unpack, behind1, gap1)
-    for b in range(4):
-        n = (0, 1, 6, 7)[b]
-        bank[1, b] = (n, mm(n, 128, "e", 128 * b, "land", 128, True, False, *[scan1[b // 2, 2 * (b % 2) + h] for h in (0, 1)]))
-    dn1 = [D("y", "dn1", T.ws1[:, 32 * h:32 * h + 32, 0], T.td1[32 * h:32 * h + 8, 16:48], tr1) for h in range(4)]
-    va = [pick("va", 128 * i, 128 * i + 128, "b1", 512, "off1", 8 * i, *of1) for i in (0, 1)]
-    send(lambda d: K("va", 32 * d, 32 * d + 32).bitcast(dt.uint8), K("hva", 32 * me, 32 * me + 32).bitcast(dt.uint8), "rva", False, va[0][0], va[1][0])
-    send(lambda d: P("va", 32 * d, 32 * d + 32), P("hva", 32 * me, 32 * me + 32), "rva", False, va[0][1], va[1][1])
-    send(lambda d: T.ws1[d], T.wl1[me], "rn1", True, *dn1)
-    qr, rc = [], {}
-    third = arrivals("rs", range(8), 2, False)
-
-    for i in (0, 1):
-        fin = [mm(bank[i, b][0], 128, *(("ne", 128 * b) if b < 3 else ("n3", 0)), "va", 128 * i, False, True, qne[min(b, 2)], *(va[i] + ((third, own3[0], own3[1]) if b == 3 else ()))) for b in range(4)]
-        for b in range(4):
-            rc[i, b] = (cp if b in ((0, 2), (2,))[i] else act)(T.rt[:, 512 * i + b:512 * i + 512:4], T["p%d" % bank[i, b][0]][:, 0:128], fin[b])
-        qr.append(quant("r", "rt", 128 * i, 128 * i + 128, 512 * i, *[rc[i, b] for b in range(4)]))
-
-    scan2, of2, mv2, tr2, do2 = level(2, "r", "b2", (2, 3, 4, 5), [[qr[0]], [qr[1]]], (qb2, qb2), lambda: None, behind2, gap2)
-    send(lambda d: T.m2[:, d:d + 1], T.wl2[me], "rn2", False, *mv2)
-    vb = pick("vb", 0, 256, "b2", 512, "off2", 0, *of2)
-    send(lambda d: K("vb", 32 * d, 32 * d + 32).bitcast(dt.uint8), K("hvb", 32 * me, 32 * me + 32).bitcast(dt.uint8), "rvb", False, vb[0])
-    send(lambda d: P("vb", 32 * d, 32 * d + 32), P("hvb", 32 * me, 32 * me + 32), "rvb", False, vb[1])
-
-    fl = [D("y", "df%d" % i, T.wrow[4 * i - 4 + h:4 * i - 3 + h, 0:256], T["wl%d" % i][:, 32 * h:32 * h + 32, 0], arrivals("rn%d" % i, range(8), 1, i == 1), late["wr"], *do)
-          for i, do in ((1, do1), (2, do2)) for h in range(4)]
-    qh = quant("h", "ht", 0, 128, 0, *late["h"])
-    qc = quant("c", "ct", 0, 128, 0, *late["c"])
-    mh = mm(5, 128, "c", 0, "h", 0, True, True, qc, qh, scan2[1, 2], scan2[1, 3])
+    def book(i, h):
+        out, in_ = T["bt%d" % i][:, 512 * h:512 * h + 512], T["br%d" % i][:]
+        if PLAN["m%d" % i][h] == "g":
+            return affine(out, in_, 0, 512, GE, 0.0, *((31, -1) if h == 0 else (-96, 1)), db[i - 1])
+        return lin(out, in_, T.qm4[:, h:h + 1], 0.0, qsel, db[i - 1])
+    qb = [[quant("b%d" % i, "bt%d" % i, 128 * h, 128 * h + 128, 512 * h, book(i, h)) for h in range(4)] for i in (1, 2)]
     qw = quant("w", "wt", 0, 128, 0, dw)
-    ka, sa = pick("hva", 32 * me, 32 * me + 32, "b1", 512, "off1", 2 * me, *of1)
-    kb, sb = pick("hvb", 32 * me, 32 * me + 32, "b2", 512, "off2", 2 * me, *of2)
-    hoff = cp(T.hoff[:], T.p5[:, 0:8], mh)
 
-    oa = pick("oa", 0, 128, "hva", 272, "hoff", 0, hoff, zc[0], zc[1], ka, sa, arrivals("rva", range(8), 2, False))
-    y1 = mm(4, 128, "w", 0, "oa", 0, True, False, qw, scan2[1, 0], scan2[1, 1], *oa)
-    D("y", "dst", T.oc[:, 0:512], K("oa", 0, 128).bitcast(dt.uint8), oa[0])
+    qco = quant("co", "zt", 0, 128, CO + 32 - 512, dco, ztm)
+    qx = quant("x", "xt", 0, 128, 0, dx)
+    zc = [D("y", "dz", f(n, 0, 32), f("co", 16, 48), qco) for n in ("hva", "hvb") for f in (KB, P)]
+    ms = mm(0, 128, "x", 0, "co", 0, True, True, qco, qx)
+    rmc = V(lambda: v.tensor_tensor_scan(T.rmc[:], T.low[:], T.p0[:, 120:128], LOW, MAX, MAX), ms, low)
+    ge = [ts(T.zt[:, M0:M0 + 32:4], T.rmc[:], T.rmc[:, 7:8], None, GE, None, rmc), ts(T.zt[:, M0 + 6:M0 + 32:4], T.rmc[:, 0:7], T.rmc[:, 7:8], None, GE, None, rmc)]
+    qm = quant("m", "zt", 0, 128, M0, *ge)
+    mr = mm(1, 128, "tr", 0, "m", 0, True, True, qm, qtr)
+    mz = [tt(T.zt[:, MZ + o:MZ + 32:4], T.zt[:, M0:M0 + 32:4], T.zt[:, M0 + 2:M0 + 32:4], SUB, *ge) for o in (0, 3)]
+    bh = ts(T.rqt[:, 512:576:2], T.zt[:, MZ:MZ + 32], hi2, None, MUL, None, ph, *mz)
+    bl = ts(T.rqt[:, 576:640:2], T.zt[:, MZ:MZ + 32], lo2, None, MUL, None, pl, *mz)
+    vl = V(lambda: v.tensor_reduce(val, T.p1[:, 0:8], AxisListType.X, MAX), mr)
+    r0 = ts(T.rqt[:, 0:512:2], T.ri[:], 256.0, val, ADD, EQ, vl, gr)
+    qrq = quant("rq", "rqt", 0, 160, 0, r0, bh, bl, rqz)
+    ml = mm(6, 128, "rq", 0, "rq", 32, False, True, after(mm(6, 128, "rq", 0, "rq", 16, True, False, qrq)))
+    loff = ts(T.loff[:], T.p6[:, 112:128], 0.5, None, MUL, None, ml)
+    for part, sem in ((far, "ra"), (near, "rb")):
+        a = 32 * min(part + [me] * (part is near))
+        sk, ss = pick("slot", a, a + 128, "x", 128, "loff", a // 16, loff)
+        for f, dep in ((KB, sk), (P, ss)):
+            send(part, "die" if f is KB else "die2", (lambda f: lambda d: f("slot", 32 * d, 32 * d + 32))(f), (lambda f: lambda d: f("land", 32 * place(d, me), 32 * place(d, me) + 32))(f), sem, dep)
+    own = pick("land", 224, 256, "x", 128, "loff", 2 * me, loff)
+
+    def turn(st, out, s1, s2, deps):
+        m = 64 * st
+        pairs = [(h, a) for h in range(4) for a in range(4) if a != h]
+        mv = [(cp if PLAN["mv%d" % st][k] == "v" else act)(T.tm[32 * h:32 * h + 32, m + 4 + a:m + 5 + a], T.tm[32 * a:32 * a + 32, m + h:m + h + 1], deps[h]) for k, (h, a) in enumerate(pairs)]
+        sw = turn32(T.tm[:, m + 32:m + 64], T.td[:, m + 16:m + 48], *[turn32(T.td[:, m + k:m + k + 32], T.tm[:, m:m + 32], *mv) for k in (0, 32)])
+        return ts(out, T.tm[:, m:m + 64].indirect(T.lt[:, 0:1]), s1, s2, ADD, None if s2 is None else MAX, sw, lt, qoff)
+
+    def look(lev, i, z, banks, zdeps):
+        L, st = str(lev), 2 * lev - 1 + i
+        rm, sg = T["rm" + L], T["sg" + L]
+        mmx = [mm(banks[j], n, z, 128 * i, "b" + L, a, True, True, *(qb[lev - 1][a // 128:(a + n) // 128] + zdeps)) for j, a, n in ((0, 0, 128), (1, 128, 384))]
+        scan = {}
+        for j in (0, 1):
+            b = "p%d" % banks[j]
+            for o, w in (((0, 128),), ((0, 128), (128, 256)))[j]:
+                c = 512 * i + 128 * j + o
+                h = V((lambda c, b, o, w: lambda: v.tensor_tensor_scan(rm[:, c:c + w], T.rs[:, 0:w], T[b][:, o:o + w], LOW, MIN, MAX))(c, b, o, w), mmx[j], rs)
+                for k in range(o // 128, (o + w) // 128):
+                    scan[j + k] = h
+        sign = [under(sg[:, c:c + 128], rm[:, c:c + 128], rm[:, c + 127:c + 128], T.tm[:, 64 * st + h:64 * st + h + 1], scan[h], tmz) for h, c in enumerate(range(512 * i, 512 * i + 512, 128))]
+        return scan, turn(st, T["off" + L][:, 16 * i:16 * i + 16], qo, None, sign)
+
+    arr = [[arrivals("ra", (far, "die"), (far, "die"))], [arrivals("rb", (near, "die"), (near, "die2")), *own]]
+    scA, ofA = look(1, 0, "land", (0, 1), arr[0] + [vl])
+    scB, ofB = look(1, 1, "land", (2, 3), arr[1])
+    banks, free = ((4, 5, 6, 7), (0, 2, 3, 1)), ([[loff]] * 4, [[scA[0]], [scB[0]], [scB[1], scB[3]], [scA[1], scA[3]]])
+    va, qr = [], []
+    for i, of in ((0, ofA), (1, ofB)):
+        dq = [mm(banks[i][b], 128, "e", 128 * b, "land", 128 * i, True, False, qe[b], *(free[i][b] + arr[i])) for b in range(4)]
+        va.append(pick("va", 128 * i, 128 * i + 128, "b1", 512, "off1", 16 * i, of))
+        fin = [mm(banks[i][b], 128, *(("ne", 128 * b) if b < 3 else ("n3", 0)), "va", 128 * i, False, True, after(dq[b]), *(va[i] + ((qne[b],) if b < 3 else (third, own3[0])))) for b in range(4)]
+        rc = [(cp if PLAN["cA" if i == 0 else "cB"][b] == "v" else act)(T.rt[:, 512 * i + b:512 * i + 512:4], T["p%d" % banks[i][b]][:, 0:128], fin[b]) for b in range(4)]
+        qr.append(quant("r", "rt", 128 * i, 128 * i + 128, 512 * i, *rc))
+
+    def col(d): return 2 * place(me, d) + 8 * (d not in far)
+    def home(n, f): return (lambda d: f(n, 32 * place(me, d), 32 * place(me, d) + 32)), (lambda d: f("h" + n, 32 + 32 * me, 64 + 32 * me))
+    def numbers(L): return (lambda d: T["off" + L][:, col(d):col(d) + 2]), (lambda d: T["wl" + L][:, 2 * me:2 * me + 2])
+    send(far + near, "all", *home("va", KB), "rva", va[0][0], va[1][0])
+    send(far + near, "all", *home("va", P), "rva", va[0][1], va[1][1])
+    send(far + near, "all", *numbers("1"), "rn1", ofA, ofB)
+    dva = [D("y", "dva", f("hva", 32 + 32 * me, 64 + 32 * me), f("va", 224, 256), dep) for f, dep in ((KB, va[1][0]), (P, va[1][1]))]
+    do1 = D("y", "do1", T.wl1[:, 2 * me:2 * me + 2], T.off1[:, col(me):col(me) + 2], ofB)
+
+    o2A, o2B = look(2, 0, "r", (4, 5), [qr[0]])[1], look(2, 1, "r", (0, 2), [qr[1]])[1]
+    for i, part, of in ((0, far, o2A), (1, near, o2B)):
+        send(part, "die", *numbers("2"), "rn2" + "ab"[i], of)
+        vb = pick("vb", 128 * i, 128 * i + 32 * len(part), "b2", 512, "off2", 16 * i, of)
+        send(part, "die", *home("vb", KB), "rvb", vb[0])
+        send(part, "die2", *home("vb", P), "rvb", vb[1])
+    do2 = D("y", "do2", T.wl2[:, 2 * me:2 * me + 2], T.off2[:, col(me):col(me) + 2], o2B)
+    kb, sb = pick("hvb", 32 + 32 * me, 64 + 32 * me, "b2", 512, "off2", col(me), o2B)
+
+    cl = under(T.sc8[:], T.rmc[:], T.rmc[:, 7:8], C("cell"), rmc)
+    hu = lin(C("hu"), C("cell"), 32.0, val, cl, vl)
+    tk = ts(C("tk"), val, 288.0, None, LT, None, vl)
+    v4 = ts(T.tm[:, 0:4], T.zt[:, Z0:Z0 + 4], C("hu"), C("tk"), ADD, MUL, hu, tk, tmz)
+    hoff = turn(0, T.hoff[:], -224.0, 0.0, [v4] * 4)
+
+    def names(L, a, b, *deps): return act(T["wr" + L][:, 32 + 16 * a:32 + 16 * b], T.nrow[:].indirect(T["wl" + L][:, a:b]), gn, *deps)
+    n1 = names("1", 0, 16, arrivals("rn1", (far + near, "all")), do1)
+    oa = pick("oa", 0, 128, "hva", 288, "hoff", 0, hoff, zc[0], arrivals("rva", (far + near, "all"), (far + near, "all")), dva[0])
+    y1 = mm(1, 128, "w", 0, "oa", 0, True, False, qw, qr[1], *oa)
+    D("y", "dst", T.oc[:, 0:512], KB("oa", 0, 128), oa[0])
     for k in range(4):
         D("y", "dst", T.osc[4 * k:4 * k + 4, 0:128], T.s_oa[32 * k:32 * k + 4, :], oa[1])
-    ob = pick("ob", 0, 128, "hvb", 272, "hoff", 0, hoff, zc[2], zc[3], kb, sb, arrivals("rvb", range(8), 2, False))
-    y2 = mm(4, 128, "w", 0, "ob", 0, False, True, *ob)
-    wn = act(T.wnf[:], T.wrow[:].indirect(T.hoff[:]), hoff, *fl)
-    D("y", "dst", T.oc[:, 512:1024], K("ob", 0, 128).bitcast(dt.uint8), ob[0])
+    n2 = [names("2", 2 * min(far), 2 * min(far) + 8, arrivals("rn2a", (far, "die")))]
+    w1 = act(T.wf1[:], T.wr1[:].indirect(T.hoff[:, 0:8]), hoff, n1, wm[0])
+    D("y", "dst", T.wn[0:4, :], T.wf1[0:128:32, :], w1)
+    n2.append(names("2", 2 * min(near + [me]), 2 * min(near + [me]) + 8, arrivals("rn2b", (near, "die")), do2))
+    ob = pick("ob", 0, 128, "hvb", 288, "hoff", 0, hoff, zc[2], kb, sb, arrivals("rvb", (far, "die"), (far, "die"), (near, "die"), (near, "die2")))
+    y2 = mm(1, 128, "w", 0, "ob", 0, False, True, after(y1), *ob)
+    w2 = act(T.wf2[:], T.wr2[:].indirect(T.hoff[:, 0:8]), hoff, wm[1], *n2)
+    D("y", "dst", T.oc[:, 512:1024], KB("ob", 0, 128), ob[0])
     for k in range(4):
         D("y", "dst", T.osc[4 * k:4 * k + 4, 128:256], T.s_ob[32 * k:32 * k + 4, :], ob[1])
-    yc = cp(T.yt[:], T.p4[:, 0:128], y2)
+    yc = cp(T.yt[:], T.p1[:, 0:128], y2)
     D("s", "dso", T.y[:], T.yt[:], yc)
-    D("y", "dst", T.wn[:], T.wnf[0:8, :], wn)
+    D("y", "dst", T.wn[4:8, :], T.wf2[0:128:32, :], w2)
 
-    total, at = {}, []
-    for q, fn, deps, sem, inc in ops:
+    order = ORDER or list(range(len(ops)))
+    total, at = {}, {}
+    for i in order:
+        sem, inc = ops[i][3], ops[i][4]
         if sem:
             total[sem] = total.get(sem, 0) + inc
-        at.append((sem, total.get(sem, 0)))
+        at[i] = (sem, total.get(sem, 0))
     total.update(expect)
-    known, most = {q: {} for q in queue}, {}
+    known, knew = {q: {} for q in queue}, {}
 
     def wait(q, sem, n):
         if known[q].get(sem, 0) < n:
             queue[q].wait_ge(T.sem[sem], n)
             known[q][sem] = n
-            most[sem] = max(most.get(sem, 0), n)
-    for q, fn, deps, sem, inc in ops:
-        need = {}
-        for d in deps:
-            s, n = d if isinstance(d, tuple) else at[d]
-            if s.startswith("d"):
-                n = total[s]
-            need[s] = max(need.get(s, 0), n)
-        for s in need:
-            wait(q, s, need[s])
+    for i in order:
+        q, fn, deps, sem, inc = ops[i]
+        need = [d if isinstance(d, tuple) else (at[d][0], total[at[d][0]]) if at[d][0].startswith("d") else at[d] for d in deps if isinstance(d, tuple) or d >= 0]
+        for s, n in need:
+            for s2, n2 in knew.get((s, n), {}).items():
+                known[q][s2] = max(known[q].get(s2, 0), n2)
+        for s in sorted(set(s for s, n in need)):
+            wait(q, s, max(n for s2, n in need if s2 == s))
         ins = fn()
         if sem:
             ins.then_inc(T.sem[sem], inc)
+            if not sem.startswith("d"):
+                knew[at[i]] = dict(known[q])
     for s in total:
-        if most.get(s, 0) < total[s]:
+        if max(known[q].get(s, 0) for q in queue) < total[s]:
             wait("g", s, total[s])

from concourse.bass import DstId, RemoteDMATransfer
from concourse.mybir import dt, AluOpType, AxisListType, ActivationFunctionType

BF, F32, U16, COD, PL = "bfloat16", "float32", "uint16", "float8_e4m3fn_x4", "uint8"
SCRATCH = {}
for _n, _w in (("xt", 512), ("wt", 512), ("br1", 512), ("br2", 512), ("bt1", 2048), ("bt2", 2048), ("et", 528), ("en", 640), ("trt", 512), ("rqt", 640), ("zt", 624), ("rt", 1024),
               ("jd", 128), ("dg", 128), ("rs", 256), ("ri", 256), ("sc8", 8), ("sg1", 1024), ("sg2", 1024), ("nrow", 512), ("wr1", 288), ("wr2", 288)):
    SCRATCH[_n] = ("sbuf", [128, _w], BF)
for _n, _w in (("low", 8), ("pc", 4), ("crow", 4), ("qm4", 4), ("ph", 4), ("pl", 4), ("pq", 4), ("qoff", 4), ("t1", 4), ("t2", 4), ("t3", 4), ("t4", 4), ("t5", 4), ("t6", 4), ("t7", 4),
               ("rmc", 8), ("val", 4), ("cell", 4), ("hu", 4), ("tk", 4), ("rm1", 1024), ("rm2", 1024), ("tm", 320), ("td", 320), ("wf1", 128), ("wf2", 128), ("yt", 128)):
    SCRATCH[_n] = ("sbuf", [128, _w], F32)
for _n, _w in (("lt", 2), ("loff", 16), ("hoff", 16), ("off1", 32), ("off2", 32), ("wl1", 16), ("wl2", 16)):
    SCRATCH[_n] = ("sbuf", [128, _w], U16)
for _n, _w in (("x", 128), ("co", 128), ("w", 128), ("b1", 512), ("b2", 512), ("e", 512), ("ne", 416), ("n3", 128), ("tr", 128), ("m", 128), ("rq", 160),
               ("slot", 256), ("land", 256), ("va", 256), ("r", 256), ("vb", 256), ("hva", 288), ("hvb", 288), ("oa", 128), ("ob", 128)):
    SCRATCH["k_" + _n] = ("sbuf", [128, _w], COD)
    SCRATCH["s_" + _n] = ("sbuf", [128, _w], PL)
for _n in range(8):
    SCRATCH["p%d" % _n] = ("psum", [128, 512], F32)
SEMAPHORES = ["cv", "cs", "ce", "cg", "dx", "dco", "db1", "db2", "dw", "do1", "do2", "dva", "dst", "dso",
              "ra", "rb", "rva", "rvb", "rn1", "rn2a", "rn2b", "rs", "dn3", "dz", "loc"]

ADD, SUB, MUL, MAX = AluOpType.add, AluOpType.subtract, AluOpType.mult, AluOpType.max
MIN, GE, EQ, LT, NE = AluOpType.min, AluOpType.is_ge, AluOpType.is_equal, AluOpType.is_lt, AluOpType.not_equal
COPY, SIGN, IDENT = ActivationFunctionType.Copy, ActivationFunctionType.Sign, ActivationFunctionType.Identity
LOW = -1e29
BIG = 1e29
SH = 14
MZ, M0, Z0, CO = 0, 32, 64, 592


def R(k):
    return 1.5 * 2.0 ** 23 * k


PLAN = {"cA": "vsvs", "cB": "svss", "m1": "ssss", "m2": "gssg", "mv0": "vsvsvsvsvsvs", "mv1": "vvsvvsvvsvvs", "mv2": "vvsvvsvvsvvs", "mv3": "vvsvvsvvsvvs", "mv4": "vvsvvsvvsvvs"}
ORDER = [0,11,1,6,2,3,4,5,10,30,7,29,41,42,25,24,12,13,26,14,43,31,71,8,72,46,17,27,77,44,16,23,20,54,22,78,21,18,47,80,79,28,68,81,45,83,60,84,82,33,32,86,87,85,56,88,48,89,36,58,90,50,91,38,92,254,252,93,94,61,253,95,49,98,97,96,51,55,102,59,52,66,99,57,69,37,100,101,34,64,62,35,255,103,104,105,53,106,108,129,107,109,19,128,65,114,111,112,113,132,110,123,131,117,120,130,135,121,116,169,136,115,119,170,118,153,122,134,67,156,168,143,133,171,125,124,154,146,144,155,148,147,145,126,142,140,139,141,265,138,137,127,149,150,158,157,261,151,267,160,259,152,162,15,161,173,172,159,164,165,184,186,177,188,163,166,76,176,73,75,175,266,187,74,260,174,181,185,167,180,179,190,63,178,183,258,264,263,189,182,9,193,214,215,192,196,191,216,197,218,195,204,194,217,208,219,207,201,202,198,209,199,203,205,200,223,206,224,222,210,211,262,220,212,233,232,221,213,227,226,225,239,228,229,231,230,234,240,257,241,235,236,242,272,237,256,238,243,268,269,249,245,246,270,251,247,271,281,250,39,70,248,282,40,273,244,274,277,275,276,279,278,280,283,286,285,284,289,287,291,290,293,292,294,288,295,296]


def rank_program(g, core, T, topo):
    me = T.rank_of(core)
    if me is None:
        return
    ops, queue = [], {"v": g.vector, "s": g.scalar, "e": g.tensor, "g": g, "y": g.sync}
    own_sem = {"v": "cv", "s": "cs", "e": "ce", "g": "cg"}

    def add(q, fn, deps=(), sem=None, inc=1):
        ops.append((q, fn, list(deps), own_sem[q] if sem is None else sem, inc))
        return len(ops) - 1

    def after(h): return -1 - h
    def V(fn, *deps): return add("v", fn, deps)
    def S(fn, *deps): return add("s", fn, deps)
    def E(fn, *deps): return add("e", fn, deps)
    def G(fn, *deps): return add("g", fn, deps)
    def D(q, sem, out, in_, *deps): return add(q, lambda: queue[q].dma_start(out, in_), deps, sem, 16)

    v, sc, te = g.vector, g.scalar, g.tensor
    K = lambda n, a, b: T["k_" + n][:, a:b]
    KB = lambda n, a, b: T["k_" + n][:, a:b].bitcast(dt.uint8)
    P = lambda n, a, b: T["s_" + n][:, a:b]
    C = lambda n: T[n][:, 0:1]

    def ts(out, in0, s1, s2, op0, op1, *deps):
        return V(lambda: v.tensor_scalar(out, in0, s1, s2, op0) if op1 is None else v.tensor_scalar(out, in0, s1, s2, op0, op1), *deps)

    def tt(out, in0, in1, op, *deps): return V(lambda: v.tensor_tensor(out, in0, in1, op), *deps)
    def cp(out, in_, *deps): return V(lambda: v.tensor_copy(out, in_), *deps)
    def turn32(out, in_, *deps): return V(lambda: v.transpose(out, in_), *deps)
    def act(out, in_, *deps): return S(lambda: sc.activation(out, in_, COPY), *deps)
    def fill(ap, c, *deps): return V(lambda: v.memset(ap, c), *deps)
    def affine(out, in_, step, n, op, f, base, cm, *deps): return G(lambda: g.affine_select(out, in_, [[step, n]], op, f, base, cm), *deps)
    def iota(out, pattern, base, cm): return G(lambda: g.iota(out, pattern, base, cm, allow_small_or_imprecise_dtypes=True))
    def lin(out, in_, a, b, *deps): return S(lambda: sc.activation(out, in_, COPY if isinstance(b, float) else IDENT, bias=b, scale=a), *deps)
    def under(out, in_, top, count, *deps): return S(lambda: sc.activation(out, in_, SIGN, bias=top, scale=-1.0, accum_out=count), *deps)

    def quant(n, tile, a, b, src, *deps):
        return V(lambda: v.quantize_mx(K(n, a, b), P(n, a, b), T[tile][:, src:src + 4 * (b - a)]), *deps)

    def mm(bank, n, w, wa, x, xa, start, stop, *deps):
        return E(lambda: te.matmul_mx(T["p%d" % bank][:, 0:n], K(w, wa, wa + 128), P(w, wa, wa + 128), K(x, xa, xa + n), P(x, xa, xa + n), start, stop), *deps)

    def pick(o, a, b, w, wn, off, c, *deps):
        k = (b - a) // 16
        return (V(lambda: v.tensor_copy(K(o, a, b).bitcast(dt.uint32), K(w, 0, wn).bitcast(dt.uint32).indirect(T[off][:, c:c + k])), *deps),
                S(lambda: sc.activation(P(o, a, b), P(w, 0, wn).indirect(T[off][:, c:c + k]), COPY), *deps))

    ranks = range(len(T.cores))

    def far_of(d): return [s for s in ranks if topo.die(T.cores[s]) != topo.die(T.cores[d])]
    def near_of(d): return [s for s in ranks if s != d and s not in far_of(d)]
    def place(d, s): return (far_of(d) + near_of(d) + [d]).index(s)
    far, near = far_of(me), near_of(me)

    def engines(s, d, form):
        e = topo.engines(T.cores[s], T.cores[d])
        w = len(e) // 4
        part = far_of(s) if d in far_of(s) else near_of(s)
        i = part.index(d)
        if form in ("die", "die2"):
            if len(part) == 4:
                return e[w * i:w * i + w]
            return [e[a * w:b * w] for a, b in (((0, 1), (1, 2), (2, 4)) if form == "die" else ((2, 3), (0, 2), (3, 4)))][i]
        e = e[0::2] if d in far_of(s) else e[1::2]
        w = len(e) // 4
        return e[w * i:] if form == "every" and i == len(part) - 1 else e[w * i:w * i + w]
    expect = {}

    def send(to, form, src, dst, sem, *deps):
        def call():
            tr = []
            for d in to:
                rid, pid, _ = topo.addr(T.cores[d])
                tr.append(RemoteDMATransfer(dst_ids=[DstId(rid=rid, pnc=pid)], dma_engine_mask=sum(1 << e for e in engines(me, d, form)), remote_sem=T.sem[sem], src=src(d), dst=dst(d)))
            return g.remote_dma_fused(tr, local_sem=T.sem["loc"])
        expect["loc"] = expect.get("loc", 0) + sum(len(engines(me, d, form)) for d in to)
        return add("g", call, deps, "")

    def arrivals(sem, *calls):
        expect[sem] = sum(len(engines(s, me, form)) for frm, form in calls for s in frm)
        return (sem, expect[sem])

    dco = D("s", "dco", T.zt[:, CO:CO + 32], T.co[:, 0:32])
    dx = D("y", "dx", T.xt[:], T.x[:])
    db = [D("y", "db1", T.br1[:], T.b1[:]), D("y", "db2", T.br2[:], T.b2[:])]
    dw = D("y", "dw", T.wt[:], T.w[:])

    gj = iota(T.jd[:], [[1, 128]], 0, -1)
    gp = iota(T.pc[:, 0:2], [[-16, 2]], -15, 2)
    gc = iota(T.crow[:], [[64, 4]], 0, 0)
    gr = iota(T.ri[:], [[0, 8], [1, 16], [16, 2]], 0, 0)
    gn = iota(T.nrow[:], [[0, 4], [1, 128]], 0, 0)
    enm = fill(T.en[:], 0.0)
    ztm = fill(T.zt[:, MZ:CO], 0.0)
    e0 = ts(T.en[:, 3:512:4], T.jd[:], 0.0, -1.0, EQ, MUL, gj, enm)
    e1 = ts(T.en[:, 516:516 + 4 * SH:4], T.jd[:, SH * me:SH * me + SH], 0.0, -1.0, EQ, MUL, gj, enm)
    e2 = ts(T.en[:, 516 + 4 * SH:580 + 4 * SH:4], T.jd[:, 8 * SH:128], 0.0, -1.0, EQ, MUL, gj, enm)
    qne = [quant("ne", "en", 128 * b, 128 * b + 128, 3 - b, e0) for b in (0, 1)] + [quant("ne", "en", 256, 400 + SH, 1, e0, e1, e2)]
    send(far + near, "every", lambda d: KB("ne", 384, 384 + SH), lambda d: KB("n3", SH * me, SH * me + SH), "rs", qne[2])
    send(far + near, "all", lambda d: P("ne", 384, 384 + SH), lambda d: P("n3", SH * me, SH * me + SH), "rs", qne[2])
    own3 = [D("y", "dn3", f("n3", a, a + n), f("ne", b, b + n), qne[2]) for f in (KB, P) for a, b, n in ((SH * me, 384, SH), (8 * SH, 384 + SH, 128 - 8 * SH))]
    third = arrivals("rs", (far + near, "every"), (far + near, "all"))
    dg = ts(T.dg[:], T.jd[:], 0.0, 256.0, EQ, MUL, gj)
    tr1s = act(T.trt[:, 1:512:2], T.zt[:, Z0:Z0 + 256], ztm)
    t0 = affine(T.trt[:, 0:512:4], T.dg[:], -1, 128, GE, 1.0, 0, 1, dg)
    t2 = lin(T.trt[:, 2:512:4], T.trt[:, 0:512:4], -1.0, 0.0, t0)
    qtr = quant("tr", "trt", 0, 128, 0, t0, tr1s, t2)
    low = fill(T.low[:], LOW)
    rqz = act(T.rqt[:, 1:640:2], T.zt[:, Z0:Z0 + 320], ztm)
    ed = lin(T.et[:, 0:516], T.en[:, 0:516], -1.0, 0.0, e0)
    qe = [quant("e", "et", 128 * b, 128 * b + 128, 3 - b, ed) for b in range(4)]
    rs = fill(T.rs[:, 0:256:128], LOW, fill(T.rs[:], BIG))
    tmz = fill(T.tm[:], 0.0)
    wm = [fill(T["wr%d" % i][:, 0:32], -1.0) for i in (1, 2)]
    hi2, lo2, val, q64, qo = C("ph"), C("pl"), C("val"), C("pq"), C("qoff")
    pq = ts(q64, T.pc[:, 1:2], R(64), R(64), ADD, SUB, gp)
    ph = ts(hi2, T.pc[:, 0:1], R(32), R(32), ADD, SUB, gp)
    pl = ts(lo2, T.pc[:, 0:1], hi2, 15.0, SUB, ADD, ph)
    qsel = ts(T.qm4[:], T.crow[:], q64, None, EQ, None, pq, gc)
    qoff = lin(qo, q64, 2.0, 0.0, pq)
    a4 = ts(C("t2"), C("t1"), R(4), R(4), ADD, SUB, lin(C("t1"), lo2, 1.0, -1.0, pl))
    swap = ts(C("t4"), C("t3"), q64, hi2, ADD, NE, ts(C("t3"), lo2, C("t2"), 16.0, SUB, MUL, a4), pq)
    diag = ts(C("t5"), C("t2"), 16.0, q64, MUL, EQ, a4, pq)
    lt = ts(T.lt[:, 0:1], C("t2"), 0.25, C("t7"), MUL, ADD, lin(C("t7"), C("t5"), -4.0, C("t6"), diag, lin(C("t6"), C("t4"), 32.0, 4.0, swap)))

    def book(i, h):
        out, in_ = T["bt%d" % i][:, 512 * h:512 * h + 512], T["br%d" % i][:]
        if PLAN["m%d" % i][h] == "g":
            return affine(out, in_, 0, 512, GE, 0.0, *((31, -1) if h == 0 else (-96, 1)), db[i - 1])
        return lin(out, in_, T.qm4[:, h:h + 1], 0.0, qsel, db[i - 1])
    qb = [[quant("b%d" % i, "bt%d" % i, 128 * h, 128 * h + 128, 512 * h, book(i, h)) for h in range(4)] for i in (1, 2)]
    qw = quant("w", "wt", 0, 128, 0, dw)

    qco = quant("co", "zt", 0, 128, CO + 32 - 512, dco, ztm)
    qx = quant("x", "xt", 0, 128, 0, dx)
    zc = [D("y", "dz", f(n, 0, 32), f("co", 16, 48), qco) for n in ("hva", "hvb") for f in (KB, P)]
    ms = mm(0, 128, "x", 0, "co", 0, True, True, qco, qx)
    rmc = V(lambda: v.tensor_tensor_scan(T.rmc[:], T.low[:], T.p0[:, 120:128], LOW, MAX, MAX), ms, low)
    ge = [ts(T.zt[:, M0:M0 + 32:4], T.rmc[:], T.rmc[:, 7:8], None, GE, None, rmc), ts(T.zt[:, M0 + 6:M0 + 32:4], T.rmc[:, 0:7], T.rmc[:, 7:8], None, GE, None, rmc)]
    qm = quant("m", "zt", 0, 128, M0, *ge)
    mr = mm(1, 128, "tr", 0, "m", 0, True, True, qm, qtr)
    mz = [tt(T.zt[:, MZ + o:MZ + 32:4], T.zt[:, M0:M0 + 32:4], T.zt[:, M0 + 2:M0 + 32:4], SUB, *ge) for o in (0, 3)]
    bh = ts(T.rqt[:, 512:576:2], T.zt[:, MZ:MZ + 32], hi2, None, MUL, None, ph, *mz)
    bl = ts(T.rqt[:, 576:640:2], T.zt[:, MZ:MZ + 32], lo2, None, MUL, None, pl, *mz)
    vl = V(lambda: v.tensor_reduce(val, T.p1[:, 0:8], AxisListType.X, MAX), mr)
    r0 = ts(T.rqt[:, 0:512:2], T.ri[:], 256.0, val, ADD, EQ, vl, gr)
    qrq = quant("rq", "rqt", 0, 160, 0, r0, bh, bl, rqz)
    ml = mm(6, 128, "rq", 0, "rq", 32, False, True, after(mm(6, 128, "rq", 0, "rq", 16, True, False, qrq)))
    loff = ts(T.loff[:], T.p6[:, 112:128], 0.5, None, MUL, None, ml)
    for part, sem in ((far, "ra"), (near, "rb")):
        a = 32 * min(part + [me] * (part is near))
        sk, ss = pick("slot", a, a + 128, "x", 128, "loff", a // 16, loff)
        for f, dep in ((KB, sk), (P, ss)):
            send(part, "die" if f is KB else "die2", (lambda f: lambda d: f("slot", 32 * d, 32 * d + 32))(f), (lambda f: lambda d: f("land", 32 * place(d, me), 32 * place(d, me) + 32))(f), sem, dep)
    own = pick("land", 224, 256, "x", 128, "loff", 2 * me, loff)

    def turn(st, out, s1, s2, deps):
        m = 64 * st
        pairs = [(h, a) for h in range(4) for a in range(4) if a != h]
        mv = [(cp if PLAN["mv%d" % st][k] == "v" else act)(T.tm[32 * h:32 * h + 32, m + 4 + a:m + 5 + a], T.tm[32 * a:32 * a + 32, m + h:m + h + 1], deps[h]) for k, (h, a) in enumerate(pairs)]
        sw = turn32(T.tm[:, m + 32:m + 64], T.td[:, m + 16:m + 48], *[turn32(T.td[:, m + k:m + k + 32], T.tm[:, m:m + 32], *mv) for k in (0, 32)])
        return ts(out, T.tm[:, m:m + 64].indirect(T.lt[:, 0:1]), s1, s2, ADD, None if s2 is None else MAX, sw, lt, qoff)

    def look(lev, i, z, banks, zdeps):
        L, st = str(lev), 2 * lev - 1 + i
        rm, sg = T["rm" + L], T["sg" + L]
        mmx = [mm(banks[j], n, z, 128 * i, "b" + L, a, True, True, *(qb[lev - 1][a // 128:(a + n) // 128] + zdeps)) for j, a, n in ((0, 0, 128), (1, 128, 384))]
        scan = {}
        for j in (0, 1):
            b = "p%d" % banks[j]
            for o, w in (((0, 128),), ((0, 128), (128, 256)))[j]:
                c = 512 * i + 128 * j + o
                h = V((lambda c, b, o, w: lambda: v.tensor_tensor_scan(rm[:, c:c + w], T.rs[:, 0:w], T[b][:, o:o + w], LOW, MIN, MAX))(c, b, o, w), mmx[j], rs)
                for k in range(o // 128, (o + w) // 128):
                    scan[j + k] = h
        sign = [under(sg[:, c:c + 128], rm[:, c:c + 128], rm[:, c + 127:c + 128], T.tm[:, 64 * st + h:64 * st + h + 1], scan[h], tmz) for h, c in enumerate(range(512 * i, 512 * i + 512, 128))]
        return scan, turn(st, T["off" + L][:, 16 * i:16 * i + 16], qo, None, sign)

    arr = [[arrivals("ra", (far, "die"), (far, "die"))], [arrivals("rb", (near, "die"), (near, "die2")), *own]]
    scA, ofA = look(1, 0, "land", (0, 1), arr[0] + [vl])
    scB, ofB = look(1, 1, "land", (2, 3), arr[1])
    banks, free = ((4, 5, 6, 7), (0, 2, 3, 1)), ([[loff]] * 4, [[scA[0]], [scB[0]], [scB[1], scB[3]], [scA[1], scA[3]]])
    va, qr = [], []
    for i, of in ((0, ofA), (1, ofB)):
        dq = [mm(banks[i][b], 128, "e", 128 * b, "land", 128 * i, True, False, qe[b], *(free[i][b] + arr[i])) for b in range(4)]
        va.append(pick("va", 128 * i, 128 * i + 128, "b1", 512, "off1", 16 * i, of))
        fin = [mm(banks[i][b], 128, *(("ne", 128 * b) if b < 3 else ("n3", 0)), "va", 128 * i, False, True, after(dq[b]), *(va[i] + ((qne[b],) if b < 3 else (third, own3[0])))) for b in range(4)]
        rc = [(cp if PLAN["cA" if i == 0 else "cB"][b] == "v" else act)(T.rt[:, 512 * i + b:512 * i + 512:4], T["p%d" % banks[i][b]][:, 0:128], fin[b]) for b in range(4)]
        qr.append(quant("r", "rt", 128 * i, 128 * i + 128, 512 * i, *rc))

    def col(d): return 2 * place(me, d) + 8 * (d not in far)
    def home(n, f): return (lambda d: f(n, 32 * place(me, d), 32 * place(me, d) + 32)), (lambda d: f("h" + n, 32 + 32 * me, 64 + 32 * me))
    def numbers(L): return (lambda d: T["off" + L][:, col(d):col(d) + 2]), (lambda d: T["wl" + L][:, 2 * me:2 * me + 2])
    send(far + near, "all", *home("va", KB), "rva", va[0][0], va[1][0])
    send(far + near, "all", *home("va", P), "rva", va[0][1], va[1][1])
    send(far + near, "all", *numbers("1"), "rn1", ofA, ofB)
    dva = [D("y", "dva", f("hva", 32 + 32 * me, 64 + 32 * me), f("va", 224, 256), dep) for f, dep in ((KB, va[1][0]), (P, va[1][1]))]
    do1 = D("y", "do1", T.wl1[:, 2 * me:2 * me + 2], T.off1[:, col(me):col(me) + 2], ofB)

    o2A, o2B = look(2, 0, "r", (4, 5), [qr[0]])[1], look(2, 1, "r", (0, 2), [qr[1]])[1]
    for i, part, of in ((0, far, o2A), (1, near, o2B)):
        send(part, "die", *numbers("2"), "rn2" + "ab"[i], of)
        vb = pick("vb", 128 * i, 128 * i + 32 * len(part), "b2", 512, "off2", 16 * i, of)
        send(part, "die", *home("vb", KB), "rvb", vb[0])
        send(part, "die2", *home("vb", P), "rvb", vb[1])
    do2 = D("y", "do2", T.wl2[:, 2 * me:2 * me + 2], T.off2[:, col(me):col(me) + 2], o2B)
    kb, sb = pick("hvb", 32 + 32 * me, 64 + 32 * me, "b2", 512, "off2", col(me), o2B)

    cl = under(T.sc8[:], T.rmc[:], T.rmc[:, 7:8], C("cell"), rmc)
    hu = lin(C("hu"), C("cell"), 32.0, val, cl, vl)
    tk = ts(C("tk"), val, 288.0, None, LT, None, vl)
    v4 = ts(T.tm[:, 0:4], T.zt[:, Z0:Z0 + 4], C("hu"), C("tk"), ADD, MUL, hu, tk, tmz)
    hoff = turn(0, T.hoff[:], -224.0, 0.0, [v4] * 4)

    def names(L, a, b, *deps): return act(T["wr" + L][:, 32 + 16 * a:32 + 16 * b], T.nrow[:].indirect(T["wl" + L][:, a:b]), gn, *deps)
    n1 = names("1", 0, 16, arrivals("rn1", (far + near, "all")), do1)
    oa = pick("oa", 0, 128, "hva", 288, "hoff", 0, hoff, zc[0], arrivals("rva", (far + near, "all"), (far + near, "all")), dva[0])
    y1 = mm(1, 128, "w", 0, "oa", 0, True, False, qw, qr[1], *oa)
    D("y", "dst", T.oc[:, 0:512], KB("oa", 0, 128), oa[0])
    for k in range(4):
        D("y", "dst", T.osc[4 * k:4 * k + 4, 0:128], T.s_oa[32 * k:32 * k + 4, :], oa[1])
    n2 = [names("2", 2 * min(far), 2 * min(far) + 8, arrivals("rn2a", (far, "die")))]
    w1 = act(T.wf1[:], T.wr1[:].indirect(T.hoff[:, 0:8]), hoff, n1, wm[0])
    D("y", "dst", T.wn[0:4, :], T.wf1[0:128:32, :], w1)
    n2.append(names("2", 2 * min(near + [me]), 2 * min(near + [me]) + 8, arrivals("rn2b", (near, "die")), do2))
    ob = pick("ob", 0, 128, "hvb", 288, "hoff", 0, hoff, zc[2], kb, sb, arrivals("rvb", (far, "die"), (far, "die"), (near, "die"), (near, "die2")))
    y2 = mm(1, 128, "w", 0, "ob", 0, False, True, after(y1), *ob)
    w2 = act(T.wf2[:], T.wr2[:].indirect(T.hoff[:, 0:8]), hoff, wm[1], *n2)
    D("y", "dst", T.oc[:, 512:1024], KB("ob", 0, 128), ob[0])
    for k in range(4):
        D("y", "dst", T.osc[4 * k:4 * k + 4, 128:256], T.s_ob[32 * k:32 * k + 4, :], ob[1])
    yc = cp(T.yt[:], T.p1[:, 0:128], y2)
    D("s", "dso", T.y[:], T.yt[:], yc)
    D("y", "dst", T.wn[4:8, :], T.wf2[0:128:32, :], w2)

    order = ORDER or list(range(len(ops)))
    total, at = {}, {}
    for i in order:
        sem, inc = ops[i][3], ops[i][4]
        if sem:
            total[sem] = total.get(sem, 0) + inc
        at[i] = (sem, total.get(sem, 0))
    total.update(expect)
    known, knew = {q: {} for q in queue}, {}

    def wait(q, sem, n):
        if known[q].get(sem, 0) < n:
            queue[q].wait_ge(T.sem[sem], n)
            known[q][sem] = n
    for i in order:
        q, fn, deps, sem, inc = ops[i]
        need = [d if isinstance(d, tuple) else (at[d][0], total[at[d][0]]) if at[d][0].startswith("d") else at[d] for d in deps if isinstance(d, tuple) or d >= 0]
        for s, n in need:
            for s2, n2 in knew.get((s, n), {}).items():
                known[q][s2] = max(known[q].get(s2, 0), n2)
        for s in sorted(set(s for s, n in need)):
            wait(q, s, max(n for s2, n in need if s2 == s))
        ins = fn()
        if sem:
            ins.then_inc(T.sem[sem], inc)
            if not sem.startswith("d"):
                knew[at[i]] = dict(known[q])
    for s in total:
        if max(known[q].get(s, 0) for q in queue) < total[s]:
            wait("g", s, total[s])
